import numpy as np
import ml_dtypes


def mxq(x, axis, fmt="e4m3"):
    dtype, down = {"e4m3": (ml_dtypes.float8_e4m3fn, 7), "e5m2": (ml_dtypes.float8_e5m2, 14)}[fmt]
    v = np.moveaxis(np.asarray(x, np.float32).astype(ml_dtypes.bfloat16).astype(np.float64), axis, -1)
    blocks = v.reshape(v.shape[:-1] + (-1, 32))
    amax = np.abs(blocks).max(-1, keepdims=True)
    byte = np.maximum(np.where(amax > 0, np.frexp(amax)[1] - 1 + 127, 0) - down, 1)
    scale = np.exp2(byte - 127.0)
    codes = (blocks / scale).astype(np.float32).astype(dtype).astype(np.float64)
    return np.moveaxis((codes * scale).reshape(v.shape), -1, axis)


WIDE = False


def mx_kscale(k):
    if not WIDE:
        return np.ones(k)
    levels = np.array([10, -10, 5, -5, 0])
    if k % 512:
        return np.exp2(np.random.permutation(np.resize(levels, k // 32))).repeat(32)
    a = np.empty((k // 512, 16))
    for p in range(k // 512):
        a[p, :8] = np.random.permutation(np.resize(levels, 8))
        for g in range(8):
            far = levels[np.abs(levels - a[p, g]) >= 10]
            a[p, g + 8] = far[np.random.randint(len(far))]
    return np.exp2(a.ravel()).repeat(32)


def f64(x):
    return np.asarray(x).astype(np.float64)


def striped(idx):
    return np.tile(idx.reshape(-1, 16).T, (8, 1)).astype(np.uint16)


def unstriped(offs):
    return offs[:16].T.reshape(-1).astype(np.int64)


K, T, E, C, N = 512, 768, 6, 256, 512
M = 512


def by_expert(wq, xq):
    return np.concatenate([wq[e].T @ xq[:, e * C:(e + 1) * C] for e in range(E)], axis=1)


def setup_inputs():
    n = np.random.standard_normal
    s = mx_kscale(K)[:, None]
    v = mx_kscale(N)
    first = np.random.permutation(np.repeat(np.arange(E), T // E))
    second = (first + 1 + np.random.permutation(np.repeat(np.arange(E - 1), -(-T // (E - 1)))[:T])) % E
    while np.bincount(second, minlength=E).max() != T // E:
        load = np.bincount(second, minlength=E); hi, lo = int(load.argmax()), int(load.argmin())
        t = np.flatnonzero((second == hi) & (first != lo))[0]; second[t] = lo
    slot_token = np.empty(E * C, np.int64); pos = np.empty((2, T), np.int64); fill = np.zeros(E, np.int64)
    place = np.stack([np.random.permutation(C) for _ in range(E)])
    for r, deal in enumerate((first, second)):
        for t in np.random.permutation(T):
            e = deal[t]; j = e * C + place[e, fill[e]]; fill[e] += 1; slot_token[j] = t; pos[r, t] = j
    g = np.random.uniform(0.2, 0.8, T)
    return {
        "xT": (n((K, T)) * s).astype(np.float32),
        "w": (n((E, K, N)) / np.sqrt(K) / s[None] * v[None, None, :]).astype(np.float32),
        "wp": (n((N, M)) / np.sqrt(N) / v[:, None]).astype(np.float32),
        "gate": np.stack([np.tile(g, (N, 1)), np.tile(1.0 - g, (N, 1))]).astype(np.float32),
        "offs": striped(slot_token),
        "pos1": striped(pos[0]),
        "pos2": striped(pos[1]),
    }


def reference(xT, w, wp, gate, offs, pos1, pos2):
    idx = unstriped(offs)
    xq = mxq(f64(xT)[:, idx], 0, "e4m3")
    y = by_expert(mxq(f64(w), 1, "e4m3"), xq)
    c = f64(gate[0]) * y[:, unstriped(pos1)] + f64(gate[1]) * y[:, unstriped(pos2)]
    return mxq(f64(wp), 0, "e4m3").T @ mxq(c, 0, "e4m3")

@@ -1,0 +1,243 @@
+from contextlib import ExitStack
+
+import concourse.mybir as mybir
+
+K, T, E, C, N, M = 512, 768, 6, 256, 512, 512
+SLOTS = E * C
+P = 128
+PACK = 4
+
+F32 = mybir.dt.float32
+BF16 = mybir.dt.bfloat16
+I32 = mybir.dt.int32
+U32 = mybir.dt.uint32
+U16 = mybir.dt.uint16
+U8 = mybir.dt.uint8
+FP8X4 = mybir.dt.float8_e4m3fn_x4
+MULT = mybir.AluOpType.mult
+ADD = mybir.AluOpType.add
+COPY = mybir.ActivationFunctionType.Copy
+
+FLOPS = 2 * SLOTS * K * N + 2 * T * N * M
+BYTES = 4 * (K * T + E * K * N + N * M + 2 * T + M * T) + 2 * (SLOTS + 2 * T)
+
+SHARES = ((96, 96), (80, 128), (72, 128), (72, 128), (72, 128), (56, 128))
+CHUNKS = (512, 256)
+X_VECTOR = (344, 168)
+
+
+def tile_moe_nxt_lin_none_kernel(tc, xT, w, wp, gate, offs, pos1, pos2, out):
+    nc = tc.nc
+    with ExitStack() as ctx:
+        lists = ctx.enter_context(tc.tile_pool(name="lists", bufs=1))
+        keep = ctx.enter_context(tc.tile_pool(name="keep", bufs=1))
+        slots = ctx.enter_context(tc.tile_pool(name="slots", bufs=2))
+        psum = ctx.enter_context(tc.psum_pool(name="psum", bufs=8))
+
+        offs_sb = lists.tile([P, SLOTS // 16], U16, name="offs_sb")
+        pos1_sb = lists.tile([P, T // 16], U16, name="pos1_sb")
+        pos2_sb = lists.tile([P, T // 16], U16, name="pos2_sb")
+
+        x_cuts = [(0, 512), (512, 256)]
+        x_view = xT.rearrange("(p j) t -> p j t", j=PACK)
+        x_raw = [keep.tile([P, PACK, n], F32, name=f"x_raw{i}") for i, (a, n) in enumerate(x_cuts)]
+        x_grp = [keep.tile([P, n, PACK], BF16, align_bytes=64, name=f"x_grp{i}") for i, (a, n) in enumerate(x_cuts)]
+        x_codes = keep.tile([P, T], U32, align_bytes=64, name="x_codes")
+        x_scales = keep.tile([P, T], U8, align_bytes=64, name="x_scales")
+        w_raw = [keep.tile([P, PACK, N], F32, name=f"w_raw{e}") for e in range(E)]
+        w_grp = [keep.tile([P, 4, P, PACK], BF16, align_bytes=64, name=f"w_grp{e}") for e in range(E)]
+        w_codes = [keep.tile([P, N], U32, align_bytes=64, name=f"w_codes{e}") for e in range(E)]
+        w_scales = [keep.tile([P, N], U8, align_bytes=64, name=f"w_scales{e}") for e in range(E)]
+        wp_raw = keep.tile([P, PACK, M], F32, name="wp_raw")
+        wp_grp = keep.tile([P, M, PACK], BF16, align_bytes=64, name="wp_grp")
+        wp_codes = keep.tile([P, M], U32, align_bytes=64, name="wp_codes")
+        wp_scales = keep.tile([P, M], U8, align_bytes=64, name="wp_scales")
+        gate_sb = keep.tile([P, 2, T], F32, name="gate_sb")
+        y = [keep.tile([P, SLOTS], F32, name=f"y{r}") for r in range(4)]
+
+        for i, (a, n) in enumerate(x_cuts):
+            nc.sync.dma_start(x_raw[i][:], x_view[:, :, a : a + n])
+            if i == 0:
+                nc.sync.dma_start(offs_sb[:], offs)
+        for e in range(E):
+            nc.sync.dma_start(w_raw[e][:], w[e].rearrange("(p j) n -> p j n", j=PACK))
+        nc.sync.dma_start(pos1_sb[:], pos1)
+        nc.sync.dma_start(pos2_sb[:], pos2)
+        nc.sync.dma_start(gate_sb[:], gate[:, 0:P, :].rearrange("g p t -> p g t"))
+        nc.sync.dma_start(wp_raw[:], wp.rearrange("(p j) m -> p j m", j=PACK))
+
+        nc.gpsimd.memset(x_scales[:], 0)
+
+        def line_view(grouped, raw):
+            return (grouped.rearrange("p (c i) j -> p c j i", i=4), raw.rearrange("p j (c i) -> p c j i", i=4))
+
+        for i, (a, n) in enumerate(x_cuts):
+            h = X_VECTOR[i]
+            o, s = line_view(x_grp[i][:, 0:h, :], x_raw[i][:, :, 0:h])
+            nc.vector.tensor_copy(o, s)
+            o, s = line_view(x_grp[i][:, h:n, :], x_raw[i][:, :, h:n])
+            nc.scalar.activation(o, s, COPY)
+        for i, (a, n) in enumerate(x_cuts):
+            nc.vector.quantize_mx(
+                out=x_codes[:, a : a + n].bitcast(FP8X4),
+                scales=x_scales[:, a : a + n],
+                in_=x_grp[i][:].rearrange("p t j -> p (t j)"),
+            )
+
+        picked = {}
+
+        def gather(e):
+            picks = offs_sb[:, e * C // 16 : (e + 2) * C // 16]
+            codes = slots.tile([P, 2 * C], U32, align_bytes=64, name="s_codes")
+            scales = slots.tile([P, 2 * C], U8, align_bytes=64, name="s_scales")
+            nc.vector.tensor_copy(codes[:], x_codes[:].indirect(picks))
+            nc.vector.tensor_copy(scales[:], x_scales[:].indirect(picks))
+            picked[e] = (codes[:, 0:C], scales[:, 0:C])
+            picked[e + 1] = (codes[:, C : 2 * C], scales[:, C : 2 * C])
+
+        def interleave_w(e):
+            s, v = SHARES[e]
+            cuts = [(0, s, 0), (s, v, 1)] + [(a, min(a + 16, P), 2) for a in range(v, P, 16)]
+            for a, b, who in cuts:
+                if a < b:
+                    o = w_grp[e][:, :, a:b, :].rearrange("p r m j -> p m j r")
+                    i = w_raw[e][:, :, 4 * a : 4 * b].rearrange("p j (m r) -> p m j r", r=4)
+                    if who == 0:
+                        nc.scalar.copy(o, i)
+                    elif who == 1:
+                        nc.vector.tensor_copy(o, i)
+                    else:
+                        nc.gpsimd.tensor_scalar(o, i, 1.0, 0.0, MULT, ADD)
+
+        def quantise_w(e, cuts):
+            for a in range(0, 4, 4 // cuts):
+                b = a + 4 // cuts
+                nc.vector.quantize_mx(
+                    out=w_codes[e][:, a * P : b * P].bitcast(FP8X4),
+                    scales=w_scales[e][:, a * P : b * P],
+                    in_=w_grp[e][:, a:b, :, :].rearrange("p r m j -> p (r m j)"),
+                )
+
+        banks = [[None] * 4 for g in range(E // 2)]
+
+        def expert(e, rows):
+            g, half = divmod(e, 2)
+            for r in rows:
+                if half == 0:
+                    banks[g][r] = psum.tile([P, 2 * C], F32, name="bank")
+                nc.tensor.matmul_mx(
+                    out=banks[g][r][:, half * C : (half + 1) * C],
+                    lhsT=w_codes[e][:, r * P : (r + 1) * P].bitcast(FP8X4),
+                    lhsT_scale=w_scales[e][:, r * P : (r + 1) * P],
+                    rhs=picked[e][0].bitcast(FP8X4),
+                    rhs_scale=picked[e][1],
+                    start=True,
+                    stop=True,
+                )
+
+        def keep_result(g, r):
+            nc.scalar.copy(y[r][:, 2 * g * C : 2 * (g + 1) * C], banks[g][r][:])
+
+        rows = range(4)
+        gather(0)
+        interleave_w(0)
+        interleave_w(1)
+        gather(2)
+        quantise_w(0, 1)
+        expert(0, rows)
+        quantise_w(1, 1)
+        expert(1, rows)
+        interleave_w(2)
+        quantise_w(2, 1)
+        expert(2, rows)
+        gather(4)
+        interleave_w(3)
+        quantise_w(3, 1)
+        expert(3, rows)
+        interleave_w(4)
+        interleave_w(5)
+        quantise_w(4, 1)
+        quantise_w(5, 2)
+        for r in rows:
+            keep_result(0, r)
+            expert(4, (r,))
+            expert(5, (r,))
+            keep_result(1, r)
+            keep_result(2, r)
+
+        o, s = line_view(wp_grp[:], wp_raw[:])
+        nc.scalar.copy(o, s)
+
+        chunks = [(sum(CHUNKS[:i]), n) for i, n in enumerate(CHUNKS)]
+        n_chunks = len(chunks)
+        parts = [[keep.tile([P, 4, n], F32, name=f"part{q}_{i}") for q in range(2)] for i, (a, n) in enumerate(chunks)]
+        c_grp = [keep.tile([P, n, 4], BF16, align_bytes=64, name=f"c_grp{i}") for i, (a, n) in enumerate(chunks)]
+        c_codes = [keep.tile([P, n], U32, align_bytes=64, name=f"c_codes{i}") for i, (a, n) in enumerate(chunks)]
+        c_scales = [keep.tile([P, n], U8, align_bytes=64, name=f"c_scales{i}") for i, (a, n) in enumerate(chunks)]
+        o_sb = [keep.tile([P, 4, n], F32, name=f"o_sb{i}") for i, (a, n) in enumerate(chunks)]
+        out_view = out.rearrange("(f p) t -> p f t", p=P)
+
+        def combine_gathers(i, rows):
+            a, n = chunks[i]
+            for r in rows:
+                for q, pos in enumerate((pos1_sb, pos2_sb)):
+                    nc.vector.tensor_tensor(
+                        parts[i][q][:, r, :],
+                        y[r][:].indirect(pos[:, a // 16 : (a + n) // 16]),
+                        gate_sb[:, q, a : a + n],
+                        MULT,
+                    )
+
+        def combine_add(i, lo, hi, r0, r1):
+            nc.vector.tensor_tensor(
+                c_grp[i][:, lo:hi, r0:r1].rearrange("p (c i) r -> p c r i", i=4),
+                parts[i][0][:, r0:r1, lo:hi].rearrange("p r (c i) -> p c r i", i=4),
+                parts[i][1][:, r0:r1, lo:hi].rearrange("p r (c i) -> p c r i", i=4),
+                ADD,
+            )
+
+        def quantise_c(i, lo, hi):
+            nc.vector.quantize_mx(
+                out=c_codes[i][:, lo:hi].bitcast(FP8X4),
+                scales=c_scales[i][:, lo:hi],
+                in_=c_grp[i][:, lo:hi, :].rearrange("p t r -> p (t r)"),
+            )
+
+        def project(i, lo, hi, engines):
+            a, n = chunks[i]
+            w_cols = hi - lo
+            for half in range(2):
+                bank = psum.tile([P, 2, w_cols], F32, name="bank")
+                for u in range(2):
+                    f = 2 * half + u
+                    nc.tensor.matmul_mx(
+                        out=bank[:, u, :],
+                        lhsT=wp_codes[:, f * P : (f + 1) * P].bitcast(FP8X4),
+                        lhsT_scale=wp_scales[:, f * P : (f + 1) * P],
+                        rhs=c_codes[i][:, lo:hi].bitcast(FP8X4),
+                        rhs_scale=c_scales[i][:, lo:hi],
+                        start=True,
+                        stop=True,
+                    )
+                engines[half](o_sb[i][:, 2 * half : 2 * half + 2, lo:hi], bank[:])
+            nc.sync.dma_start(out_view[:, :, a + lo : a + hi], o_sb[i][:, :, lo:hi])
+
+        combine_gathers(0, (0, 1, 2, 3))
+        nc.vector.quantize_mx(
+            out=wp_codes[:].bitcast(FP8X4), scales=wp_scales[:], in_=wp_grp[:].rearrange("p m j -> p (m j)")
+        )
+        combine_gathers(1, (0,))
+        combine_add(0, 0, 512, 0, 4)
+        combine_gathers(1, (1,))
+        quantise_c(0, 0, 512)
+        project(0, 0, 256, (nc.scalar.copy, nc.scalar.copy))
+        project(0, 256, 512, (nc.scalar.copy, nc.scalar.copy))
+        combine_gathers(1, (2,))
+        combine_add(1, 0, 256, 0, 2)
+        combine_gathers(1, (3,))
+        combine_add(1, 0, 128, 2, 4)
+        combine_add(1, 128, 256, 2, 4)
+        quantise_c(1, 0, 128)
+        quantise_c(1, 128, 256)
+        project(1, 0, 128, (nc.scalar.copy, nc.vector.tensor_copy))
+        project(1, 128, 256, (nc.scalar.copy, nc.vector.tensor_copy))

@@ -1,29 +1,29 @@
 from contextlib import ExitStack
 
 import concourse.mybir as mybir
+from concourse.masks import make_identity
 
 K, T, E, C, N, M = 512, 768, 6, 256, 512, 512
 SLOTS = E * C
 P = 128
 PACK = 4
+HALF = N // 2
 
 F32 = mybir.dt.float32
 BF16 = mybir.dt.bfloat16
-I32 = mybir.dt.int32
 U32 = mybir.dt.uint32
 U16 = mybir.dt.uint16
 U8 = mybir.dt.uint8
 FP8X4 = mybir.dt.float8_e4m3fn_x4
 MULT = mybir.AluOpType.mult
-ADD = mybir.AluOpType.add
 COPY = mybir.ActivationFunctionType.Copy
 
 FLOPS = 2 * SLOTS * K * N + 2 * T * N * M
 BYTES = 4 * (K * T + E * K * N + N * M + 2 * T + M * T) + 2 * (SLOTS + 2 * T)
 
-SHARES = ((96, 96), (80, 128), (72, 128), (72, 128), (72, 128), (56, 128))
-CHUNKS = (512, 256)
-X_VECTOR = (344, 168)
+X_PIECE = 256
+X_VECTOR = 160
+GROUPS = ((0, 256), (256, 256), (512, 128), (640, 128))
 
 
 def tile_moe_nxt_lin_none_kernel(tc, xT, w, wp, gate, offs, pos1, pos2, out):
@@ -31,213 +31,242 @@ def tile_moe_nxt_lin_none_kernel(tc, xT, w, wp, gate, offs, pos1, pos2, out):
     with ExitStack() as ctx:
         lists = ctx.enter_context(tc.tile_pool(name="lists", bufs=1))
         keep = ctx.enter_context(tc.tile_pool(name="keep", bufs=1))
-        slots = ctx.enter_context(tc.tile_pool(name="slots", bufs=2))
-        psum = ctx.enter_context(tc.psum_pool(name="psum", bufs=8))
+        banks = ctx.enter_context(tc.psum_pool(name="banks", bufs=6))
+        turns = ctx.enter_context(tc.psum_pool(name="turns", bufs=2))
 
         offs_sb = lists.tile([P, SLOTS // 16], U16, name="offs_sb")
-        pos1_sb = lists.tile([P, T // 16], U16, name="pos1_sb")
-        pos2_sb = lists.tile([P, T // 16], U16, name="pos2_sb")
+        pos_sb = [lists.tile([P, T // 16], U16, name=f"pos{q}_sb") for q in range(2)]
 
-        x_cuts = [(0, 512), (512, 256)]
+        n_x = T // X_PIECE
         x_view = xT.rearrange("(p j) t -> p j t", j=PACK)
-        x_raw = [keep.tile([P, PACK, n], F32, name=f"x_raw{i}") for i, (a, n) in enumerate(x_cuts)]
-        x_grp = [keep.tile([P, n, PACK], BF16, align_bytes=64, name=f"x_grp{i}") for i, (a, n) in enumerate(x_cuts)]
+        x_raw = [keep.tile([P, PACK, X_PIECE], F32, name=f"x_raw{i}") for i in range(n_x)]
+        x_grp = [keep.tile([P, X_PIECE, PACK], BF16, align_bytes=64, name=f"x_grp{i}") for i in range(n_x)]
         x_codes = keep.tile([P, T], U32, align_bytes=64, name="x_codes")
         x_scales = keep.tile([P, T], U8, align_bytes=64, name="x_scales")
-        w_raw = [keep.tile([P, PACK, N], F32, name=f"w_raw{e}") for e in range(E)]
-        w_grp = [keep.tile([P, 4, P, PACK], BF16, align_bytes=64, name=f"w_grp{e}") for e in range(E)]
-        w_codes = [keep.tile([P, N], U32, align_bytes=64, name=f"w_codes{e}") for e in range(E)]
-        w_scales = [keep.tile([P, N], U8, align_bytes=64, name=f"w_scales{e}") for e in range(E)]
-        wp_raw = keep.tile([P, PACK, M], F32, name="wp_raw")
+        w_raw = [[keep.tile([P, PACK, HALF], F32, align_bytes=64, name=f"w_raw{h}_{e}") for e in range(E)] for h in range(2)]
+        w_codes = [[keep.tile([P, HALF], U32, align_bytes=64, name=f"w_codes{h}_{e}") for e in range(E)] for h in range(2)]
+        w_scales = [[keep.tile([P, HALF], U8, align_bytes=64, name=f"w_scales{h}_{e}") for e in range(E)] for h in range(2)]
+        wp_raw = keep.tile([P, PACK, M], F32, align_bytes=64, name="wp_raw")
         wp_grp = keep.tile([P, M, PACK], BF16, align_bytes=64, name="wp_grp")
         wp_codes = keep.tile([P, M], U32, align_bytes=64, name="wp_codes")
         wp_scales = keep.tile([P, M], U8, align_bytes=64, name="wp_scales")
         gate_sb = keep.tile([P, 2, T], F32, name="gate_sb")
         y = [keep.tile([P, SLOTS], F32, name=f"y{r}") for r in range(4)]
+        ident = keep.tile([P, P], F32, name="ident")
 
-        for i, (a, n) in enumerate(x_cuts):
-            nc.sync.dma_start(x_raw[i][:], x_view[:, :, a : a + n])
-            if i == 0:
-                nc.sync.dma_start(offs_sb[:], offs)
+        def load_w(h, e):
+            nc.sync.dma_start(w_raw[h][e][:], w[e].rearrange("(p j) n -> p j n", j=PACK)[:, :, h * HALF : (h + 1) * HALF])
+
+        for i in range(n_x):
+            nc.sync.dma_start(x_raw[i][:], x_view[:, :, i * X_PIECE : (i + 1) * X_PIECE])
+        nc.sync.dma_start(offs_sb[:], offs)
         for e in range(E):
-            nc.sync.dma_start(w_raw[e][:], w[e].rearrange("(p j) n -> p j n", j=PACK))
-        nc.sync.dma_start(pos1_sb[:], pos1)
-        nc.sync.dma_start(pos2_sb[:], pos2)
+            load_w(0, e)
+        load_w(1, 0)
+        load_w(1, 1)
+        nc.sync.dma_start(pos_sb[0][:], pos1)
+        nc.sync.dma_start(pos_sb[1][:], pos2)
         nc.sync.dma_start(gate_sb[:], gate[:, 0:P, :].rearrange("g p t -> p g t"))
+        for e in range(2, E):
+            load_w(1, e)
         nc.sync.dma_start(wp_raw[:], wp.rearrange("(p j) m -> p j m", j=PACK))
 
         nc.gpsimd.memset(x_scales[:], 0)
+        make_identity(nc, ident[:])
 
         def line_view(grouped, raw):
             return (grouped.rearrange("p (c i) j -> p c j i", i=4), raw.rearrange("p j (c i) -> p c j i", i=4))
 
-        for i, (a, n) in enumerate(x_cuts):
-            h = X_VECTOR[i]
-            o, s = line_view(x_grp[i][:, 0:h, :], x_raw[i][:, :, 0:h])
+        for i in range(n_x):
+            o, s = line_view(x_grp[i][:, 0:X_VECTOR, :], x_raw[i][:, :, 0:X_VECTOR])
             nc.vector.tensor_copy(o, s)
-            o, s = line_view(x_grp[i][:, h:n, :], x_raw[i][:, :, h:n])
+            o, s = line_view(x_grp[i][:, X_VECTOR:X_PIECE, :], x_raw[i][:, :, X_VECTOR:X_PIECE])
             nc.scalar.activation(o, s, COPY)
-        for i, (a, n) in enumerate(x_cuts):
             nc.vector.quantize_mx(
-                out=x_codes[:, a : a + n].bitcast(FP8X4),
-                scales=x_scales[:, a : a + n],
+                out=x_codes[:, i * X_PIECE : (i + 1) * X_PIECE].bitcast(FP8X4),
+                scales=x_scales[:, i * X_PIECE : (i + 1) * X_PIECE],
                 in_=x_grp[i][:].rearrange("p t j -> p (t j)"),
             )
 
-        picked = {}
+        s_codes, s_scales = {}, {}
 
-        def gather(e):
-            picks = offs_sb[:, e * C // 16 : (e + 2) * C // 16]
-            codes = slots.tile([P, 2 * C], U32, align_bytes=64, name="s_codes")
-            scales = slots.tile([P, 2 * C], U8, align_bytes=64, name="s_scales")
-            nc.vector.tensor_copy(codes[:], x_codes[:].indirect(picks))
-            nc.vector.tensor_copy(scales[:], x_scales[:].indirect(picks))
-            picked[e] = (codes[:, 0:C], scales[:, 0:C])
-            picked[e + 1] = (codes[:, C : 2 * C], scales[:, C : 2 * C])
+        def gather_codes(g, tag):
+            s_codes[g] = keep.tile([P, 2 * C], U32, align_bytes=64, tag=tag, name=f"s_codes{g}")
+            nc.vector.tensor_copy(s_codes[g][:], x_codes[:].indirect(offs_sb[:, g * 32 : (g + 1) * 32]))
 
-        def interleave_w(e):
-            s, v = SHARES[e]
-            cuts = [(0, s, 0), (s, v, 1)] + [(a, min(a + 16, P), 2) for a in range(v, P, 16)]
-            for a, b, who in cuts:
-                if a < b:
-                    o = w_grp[e][:, :, a:b, :].rearrange("p r m j -> p m j r")
-                    i = w_raw[e][:, :, 4 * a : 4 * b].rearrange("p j (m r) -> p m j r", r=4)
-                    if who == 0:
-                        nc.scalar.copy(o, i)
-                    elif who == 1:
-                        nc.vector.tensor_copy(o, i)
-                    else:
-                        nc.gpsimd.tensor_scalar(o, i, 1.0, 0.0, MULT, ADD)
+        def gather_scales(g, tag):
+            s_scales[g] = keep.tile([P, 2 * C], U8, align_bytes=64, tag=tag, name=f"s_scales{g}")
+            nc.vector.tensor_copy(s_scales[g][:], x_scales[:].indirect(offs_sb[:, g * 32 : (g + 1) * 32]))
 
-        def quantise_w(e, cuts):
-            for a in range(0, 4, 4 // cuts):
-                b = a + 4 // cuts
-                nc.vector.quantize_mx(
-                    out=w_codes[e][:, a * P : b * P].bitcast(FP8X4),
-                    scales=w_scales[e][:, a * P : b * P],
-                    in_=w_grp[e][:, a:b, :, :].rearrange("p r m j -> p (r m j)"),
-                )
+        def prepare_w(h, e, engine, tag="w_grp", bufs=4):
+            grouped = keep.tile([P, HALF, PACK], BF16, align_bytes=64, tag=tag, bufs=bufs, name=f"w_grp{h}_{e}")
+            o, s = line_view(grouped[:], w_raw[h][e][:])
+            engine(o, s)
+            nc.vector.quantize_mx(
+                out=w_codes[h][e][:].bitcast(FP8X4), scales=w_scales[h][e][:], in_=grouped[:].rearrange("p n j -> p (n j)")
+            )
 
-        banks = [[None] * 4 for g in range(E // 2)]
+        y_banks = {}
 
-        def expert(e, rows):
-            g, half = divmod(e, 2)
-            for r in rows:
-                if half == 0:
-                    banks[g][r] = psum.tile([P, 2 * C], F32, name="bank")
-                nc.tensor.matmul_mx(
-                    out=banks[g][r][:, half * C : (half + 1) * C],
-                    lhsT=w_codes[e][:, r * P : (r + 1) * P].bitcast(FP8X4),
-                    lhsT_scale=w_scales[e][:, r * P : (r + 1) * P],
-                    rhs=picked[e][0].bitcast(FP8X4),
-                    rhs_scale=picked[e][1],
-                    start=True,
-                    stop=True,
-                )
-
-        def keep_result(g, r):
-            nc.scalar.copy(y[r][:, 2 * g * C : 2 * (g + 1) * C], banks[g][r][:])
-
-        rows = range(4)
-        gather(0)
-        interleave_w(0)
-        interleave_w(1)
-        gather(2)
-        quantise_w(0, 1)
-        expert(0, rows)
-        quantise_w(1, 1)
-        expert(1, rows)
-        interleave_w(2)
-        quantise_w(2, 1)
-        expert(2, rows)
-        gather(4)
-        interleave_w(3)
-        quantise_w(3, 1)
-        expert(3, rows)
-        interleave_w(4)
-        interleave_w(5)
-        quantise_w(4, 1)
-        quantise_w(5, 2)
-        for r in rows:
-            keep_result(0, r)
-            expert(4, (r,))
-            expert(5, (r,))
-            keep_result(1, r)
-            keep_result(2, r)
-
-        o, s = line_view(wp_grp[:], wp_raw[:])
-        nc.scalar.copy(o, s)
-
-        chunks = [(sum(CHUNKS[:i]), n) for i, n in enumerate(CHUNKS)]
-        n_chunks = len(chunks)
-        parts = [[keep.tile([P, 4, n], F32, name=f"part{q}_{i}") for q in range(2)] for i, (a, n) in enumerate(chunks)]
-        c_grp = [keep.tile([P, n, 4], BF16, align_bytes=64, name=f"c_grp{i}") for i, (a, n) in enumerate(chunks)]
-        c_codes = [keep.tile([P, n], U32, align_bytes=64, name=f"c_codes{i}") for i, (a, n) in enumerate(chunks)]
-        c_scales = [keep.tile([P, n], U8, align_bytes=64, name=f"c_scales{i}") for i, (a, n) in enumerate(chunks)]
-        o_sb = [keep.tile([P, 4, n], F32, name=f"o_sb{i}") for i, (a, n) in enumerate(chunks)]
-        out_view = out.rearrange("(f p) t -> p f t", p=P)
-
-        def combine_gathers(i, rows):
-            a, n = chunks[i]
-            for r in rows:
-                for q, pos in enumerate((pos1_sb, pos2_sb)):
-                    nc.vector.tensor_tensor(
-                        parts[i][q][:, r, :],
-                        y[r][:].indirect(pos[:, a // 16 : (a + n) // 16]),
-                        gate_sb[:, q, a : a + n],
-                        MULT,
+        def experts(h, g):
+            for i in range(2):
+                bank = banks.tile([P, 2 * C], F32, name="bank")
+                y_banks[2 * h + i, g] = bank
+                for half in range(2):
+                    e = 2 * g + half
+                    nc.tensor.matmul_mx(
+                        out=bank[:, half * C : (half + 1) * C],
+                        lhsT=w_codes[h][e][:, i * P : (i + 1) * P].bitcast(FP8X4),
+                        lhsT_scale=w_scales[h][e][:, i * P : (i + 1) * P],
+                        rhs=s_codes[g][:, half * C : (half + 1) * C].bitcast(FP8X4),
+                        rhs_scale=s_scales[g][:, half * C : (half + 1) * C],
+                        start=True,
+                        stop=True,
                     )
 
-        def combine_add(i, lo, hi, r0, r1):
-            nc.vector.tensor_tensor(
-                c_grp[i][:, lo:hi, r0:r1].rearrange("p (c i) r -> p c r i", i=4),
-                parts[i][0][:, r0:r1, lo:hi].rearrange("p r (c i) -> p c r i", i=4),
-                parts[i][1][:, r0:r1, lo:hi].rearrange("p r (c i) -> p c r i", i=4),
-                ADD,
-            )
+        def keep_results(h, pairs):
+            for g in pairs:
+                for r in (2 * h, 2 * h + 1):
+                    nc.scalar.copy(y[r][:, 2 * g * C : 2 * (g + 1) * C], y_banks[r, g][:])
 
-        def quantise_c(i, lo, hi):
-            nc.vector.quantize_mx(
-                out=c_codes[i][:, lo:hi].bitcast(FP8X4),
-                scales=c_scales[i][:, lo:hi],
-                in_=c_grp[i][:, lo:hi, :].rearrange("p t r -> p (t r)"),
-            )
+        def gated(part, r, a, n):
+            for q in range(2):
+                nc.vector.tensor_tensor(
+                    part[:, q, :], y[r][:].indirect(pos_sb[q][:, a // 16 : (a + n) // 16]), gate_sb[:, q, a : a + n], MULT
+                )
 
-        def project(i, lo, hi, engines):
-            a, n = chunks[i]
-            w_cols = hi - lo
+        def turn_and_add(parts, n, tag="turn"):
+            bank = turns.tile([P, n // P, HALF], F32, tag=tag, name="turn")
+            for i in range(2):
+                for b in range(n // P):
+                    for q in range(2):
+                        nc.tensor.matmul(
+                            bank[:, b, i * P : (i + 1) * P],
+                            parts[i][:, q, b * P : (b + 1) * P],
+                            ident[:],
+                            start=(q == 0),
+                            stop=(q == 1),
+                            is_transpose=True,
+                        )
+            return bank
+
+        c_rows = [keep.tile([P, n // P, 2, P, 2], BF16, name=f"c_rows{i}") for i, (a, n) in enumerate(GROUPS)]
+
+        def round_c(i, h, bank, engine):
+            engine(c_rows[i][:, :, :, 64 * h : 64 * (h + 1), :], bank.rearrange("t b (m u v) -> t b u m v", u=2, v=2))
+
+        gather_codes(0, "codes0")
+        gather_scales(0, "scales0")
+        prepare_w(0, 0, nc.scalar.copy)
+        gather_codes(1, "w_raw0_0")
+        prepare_w(0, 1, nc.scalar.copy)
+        experts(0, 0)
+        gather_scales(1, "w_raw0_1")
+        prepare_w(0, 2, nc.scalar.copy)
+        prepare_w(0, 3, nc.scalar.copy)
+        gather_codes(2, "w_raw0_3")
+        experts(0, 1)
+        prepare_w(0, 4, nc.scalar.copy)
+        gather_scales(2, "w_raw0_4")
+        prepare_w(0, 5, nc.scalar.copy)
+        experts(0, 2)
+        keep_results(0, (0, 1))
+        prepare_w(1, 0, nc.vector.tensor_copy, tag="w_raw0_5", bufs=1)
+        prepare_w(1, 1, nc.scalar.copy)
+        keep_results(0, (2,))
+
+        early = {}
+        for r in range(2):
+            early[0, r] = keep.tile([P, 2, 256], F32, name=f"early0_{r}")
+            gated(early[0, r], r, 0, 256)
+        experts(1, 0)
+        prepare_w(1, 2, nc.scalar.copy)
+        early[1, 0] = keep.tile([P, 2, 256], F32, align_bytes=64, tag="w_raw1_2", name="early1_0")
+        gated(early[1, 0], 0, 256, 256)
+        prepare_w(1, 3, nc.scalar.copy)
+        experts(1, 1)
+        early[1, 1] = keep.tile([P, 2, 256], F32, align_bytes=64, tag="w_raw1_3", name="early1_1")
+        gated(early[1, 1], 1, 256, 256)
+        prepare_w(1, 4, nc.scalar.copy)
+        prepare_w(1, 5, nc.scalar.copy)
+        experts(1, 2)
+        last = keep.tile([P, 2, 2, 256], F32, align_bytes=64, tag="w_raw1_5", name="early2")
+        for r in range(2):
+            early[2, r] = last[:, r, :, :]
+            gated(early[2, r], r, 512, 256)
+        keep_results(1, (0, 1, 2))
+
+        for s in range(2):
+            round_c(s, 0, turn_and_add([early[s, 0], early[s, 1]], 256)[:], nc.scalar.copy)
+        o, s = line_view(wp_grp[:], wp_raw[:])
+        nc.scalar.copy(o, s)
+        bank = turn_and_add([early[2, 0], early[2, 1]], 256)
+        round_c(2, 0, bank[:, 0:1, :], nc.scalar.copy)
+        round_c(3, 0, bank[:, 1:2, :], nc.scalar.copy)
+
+        c_codes = [keep.tile([P, n], U32, align_bytes=64, name=f"c_codes{i}") for i, (a, n) in enumerate(GROUPS)]
+        c_scales = [keep.tile([P, n], U8, align_bytes=64, name=f"c_scales{i}") for i, (a, n) in enumerate(GROUPS)]
+        o_sb = [keep.tile([P, 4, n], F32, name=f"o_sb{i}") for i, (a, n) in enumerate(GROUPS)]
+        out_view = out.rearrange("(f p) t -> p f t", p=P)
+        late = {}
+        c_grp = {}
+
+        def combine(i, r, tag):
+            a, n = GROUPS[i]
+            late[i, r] = keep.tile([P, 2, n], F32, align_bytes=64, tag=tag, name=f"late{i}_{r}")
+            gated(late[i, r], r, a, n)
+
+        def turn_back(i, engine):
+            a, n = GROUPS[i]
+            round_c(i, 1, turn_and_add([late[i, 2], late[i, 3]], n)[:], engine)
+            words = c_rows[i][:].rearrange("t b u p v -> t (b u p v)").bitcast(F32)
+            bank = banks.tile([P, n // P, 2, P], F32, name="bank")
+            for b in range(n // P):
+                for u in range(2):
+                    nc.tensor.transpose(bank[:, b, u, :], words[:, (2 * b + u) * P : (2 * b + u + 1) * P], ident[:])
+            for b in range(n // P):
+                c_grp[i, b] = keep.tile([P, P * PACK], BF16, align_bytes=64, name=f"c_grp{i}_{b}")
+                engine(c_grp[i, b][:].bitcast(F32).rearrange("p (t u) -> p t u", u=2), bank[:, b, :, :].rearrange("p u t -> p t u"))
+
+        def project(i, engines):
+            a, n = GROUPS[i]
+            for b in range(n // P):
+                cols = slice(b * P, (b + 1) * P)
+                nc.vector.quantize_mx(out=c_codes[i][:, cols].bitcast(FP8X4), scales=c_scales[i][:, cols], in_=c_grp[i, b][:])
             for half in range(2):
-                bank = psum.tile([P, 2, w_cols], F32, name="bank")
+                bank = banks.tile([P, 2, n], F32, name="bank")
                 for u in range(2):
                     f = 2 * half + u
                     nc.tensor.matmul_mx(
                         out=bank[:, u, :],
                         lhsT=wp_codes[:, f * P : (f + 1) * P].bitcast(FP8X4),
                         lhsT_scale=wp_scales[:, f * P : (f + 1) * P],
-                        rhs=c_codes[i][:, lo:hi].bitcast(FP8X4),
-                        rhs_scale=c_scales[i][:, lo:hi],
+                        rhs=c_codes[i][:].bitcast(FP8X4),
+                        rhs_scale=c_scales[i][:],
                         start=True,
                         stop=True,
                     )
-                engines[half](o_sb[i][:, 2 * half : 2 * half + 2, lo:hi], bank[:])
-            nc.sync.dma_start(out_view[:, :, a + lo : a + hi], o_sb[i][:, :, lo:hi])
+                engines[half](o_sb[i][:, 2 * half : 2 * half + 2, :], bank[:])
+            nc.sync.dma_start(out_view[:, :, a : a + n], o_sb[i][:])
 
-        combine_gathers(0, (0, 1, 2, 3))
+        for r in (2, 3):
+            combine(0, r, f"late0_{r}")
         nc.vector.quantize_mx(
             out=wp_codes[:].bitcast(FP8X4), scales=wp_scales[:], in_=wp_grp[:].rearrange("p m j -> p (m j)")
         )
-        combine_gathers(1, (0,))
-        combine_add(0, 0, 512, 0, 4)
-        combine_gathers(1, (1,))
-        quantise_c(0, 0, 512)
-        project(0, 0, 256, (nc.scalar.copy, nc.scalar.copy))
-        project(0, 256, 512, (nc.scalar.copy, nc.scalar.copy))
-        combine_gathers(1, (2,))
-        combine_add(1, 0, 256, 0, 2)
-        combine_gathers(1, (3,))
-        combine_add(1, 0, 128, 2, 4)
-        combine_add(1, 128, 256, 2, 4)
-        quantise_c(1, 0, 128)
-        quantise_c(1, 128, 256)
-        project(1, 0, 128, (nc.scalar.copy, nc.vector.tensor_copy))
-        project(1, 128, 256, (nc.scalar.copy, nc.vector.tensor_copy))
+        second = keep.tile([P, 2, 2, 256], F32, align_bytes=64, tag="wp_raw", name="late1")
+        for r in (2, 3):
+            late[1, r] = second[:, r - 2, :, :]
+            gated(late[1, r], r, 256, 256)
+        turn_back(0, nc.scalar.copy)
+        project(0, (nc.scalar.copy, nc.scalar.copy))
+        both = keep.tile([P, 4, 2, P], F32, align_bytes=64, tag="c_grp0_0", name="late_both")
+        for k, (i, r) in enumerate(((2, 2), (2, 3), (3, 2), (3, 3))):
+            late[i, r] = both[:, k, :, :]
+            gated(late[i, r], r, GROUPS[i][0], P)
+        turn_back(1, nc.scalar.copy)
+        turn_back(2, nc.scalar.copy)
+        project(1, (nc.scalar.copy, nc.scalar.copy))
+        turn_back(3, nc.vector.tensor_copy)
+        project(2, (nc.scalar.copy, nc.scalar.copy))
+        project(3, (nc.scalar.copy, nc.vector.tensor_copy))

@@ -21,6 +21,8 @@ COPY = mybir.ActivationFunctionType.Copy
 FLOPS = 2 * SLOTS * K * N + 2 * T * N * M
 BYTES = 4 * (K * T + E * K * N + N * M + 2 * T + M * T) + 2 * (SLOTS + 2 * T)
 
+RAW_BYTES = 4 * PACK * HALF
+Y_BYTES = 4 * SLOTS
 X_PIECE = 256
 X_VECTOR = 160
 GROUPS = ((0, 256), (256, 256), (512, 128), (640, 128))
@@ -31,8 +33,9 @@ def tile_moe_nxt_lin_none_kernel(tc, xT, w, wp, gate, offs, pos1, pos2, out):
     with ExitStack() as ctx:
         lists = ctx.enter_context(tc.tile_pool(name="lists", bufs=1))
         keep = ctx.enter_context(tc.tile_pool(name="keep", bufs=1))
+        placed = ctx.enter_context(tc.tile_pool(name="placed", bufs=1))
         banks = ctx.enter_context(tc.psum_pool(name="banks", bufs=6))
-        turns = ctx.enter_context(tc.psum_pool(name="turns", bufs=2))
+        turns = ctx.enter_context(tc.psum_pool(name="turns", bufs=1))
 
         offs_sb = lists.tile([P, SLOTS // 16], U16, name="offs_sb")
         pos_sb = [lists.tile([P, T // 16], U16, name=f"pos{q}_sb") for q in range(2)]
@@ -43,7 +46,22 @@ def tile_moe_nxt_lin_none_kernel(tc, xT, w, wp, gate, offs, pos1, pos2, out):
         x_grp = [keep.tile([P, X_PIECE, PACK], BF16, align_bytes=64, name=f"x_grp{i}") for i in range(n_x)]
         x_codes = keep.tile([P, T], U32, align_bytes=64, name="x_codes")
         x_scales = keep.tile([P, T], U8, align_bytes=64, name="x_scales")
-        w_raw = [[keep.tile([P, PACK, HALF], F32, align_bytes=64, name=f"w_raw{h}_{e}") for e in range(E)] for h in range(2)]
+        raw_at, y_at, at = {}, {}, 0
+        for h in range(2):
+            for e in range(E):
+                if e == 4:
+                    y_at[2 * h] = at
+                    at = at + Y_BYTES - 64
+                raw_at[h, e] = at
+                at = at + RAW_BYTES
+                if e == 4:
+                    y_at[2 * h + 1] = at - 64
+                    at = at + Y_BYTES - 64
+
+        def on_raw(h, e, shape, dtype, name, skip=0):
+            return placed.tile(shape, dtype, align_bytes=64, offset=raw_at[h, e] + skip, name=name)
+
+        w_raw = [[on_raw(h, e, [P, PACK, HALF], F32, f"w_raw{h}_{e}") for e in range(E)] for h in range(2)]
         w_codes = [[keep.tile([P, HALF], U32, align_bytes=64, name=f"w_codes{h}_{e}") for e in range(E)] for h in range(2)]
         w_scales = [[keep.tile([P, HALF], U8, align_bytes=64, name=f"w_scales{h}_{e}") for e in range(E)] for h in range(2)]
         wp_raw = keep.tile([P, PACK, M], F32, align_bytes=64, name="wp_raw")
@@ -51,7 +69,7 @@ def tile_moe_nxt_lin_none_kernel(tc, xT, w, wp, gate, offs, pos1, pos2, out):
         wp_codes = keep.tile([P, M], U32, align_bytes=64, name="wp_codes")
         wp_scales = keep.tile([P, M], U8, align_bytes=64, name="wp_scales")
         gate_sb = keep.tile([P, 2, T], F32, name="gate_sb")
-        y = [keep.tile([P, SLOTS], F32, name=f"y{r}") for r in range(4)]
+        y = [placed.tile([P, SLOTS], F32, align_bytes=64, offset=y_at[r], name=f"y{r}") for r in range(4)]
         ident = keep.tile([P, P], F32, name="ident")
 
         def load_w(h, e):
@@ -90,16 +108,17 @@ def tile_moe_nxt_lin_none_kernel(tc, xT, w, wp, gate, offs, pos1, pos2, out):
 
         s_codes, s_scales = {}, {}
 
-        def gather_codes(g, tag):
-            s_codes[g] = keep.tile([P, 2 * C], U32, align_bytes=64, tag=tag, name=f"s_codes{g}")
+        def gather_codes(g, tile):
+            s_codes[g] = tile
             nc.vector.tensor_copy(s_codes[g][:], x_codes[:].indirect(offs_sb[:, g * 32 : (g + 1) * 32]))
 
-        def gather_scales(g, tag):
-            s_scales[g] = keep.tile([P, 2 * C], U8, align_bytes=64, tag=tag, name=f"s_scales{g}")
+        def gather_scales(g, tile):
+            s_scales[g] = tile
             nc.vector.tensor_copy(s_scales[g][:], x_scales[:].indirect(offs_sb[:, g * 32 : (g + 1) * 32]))
 
-        def prepare_w(h, e, engine, tag="w_grp", bufs=4):
-            grouped = keep.tile([P, HALF, PACK], BF16, align_bytes=64, tag=tag, bufs=bufs, name=f"w_grp{h}_{e}")
+        def prepare_w(h, e, engine, grouped=None):
+            if grouped is None:
+                grouped = keep.tile([P, HALF, PACK], BF16, align_bytes=64, tag="w_grp", bufs=4, name=f"w_grp{h}_{e}")
             o, s = line_view(grouped[:], w_raw[h][e][:])
             engine(o, s)
             nc.vector.quantize_mx(
@@ -135,8 +154,8 @@ def tile_moe_nxt_lin_none_kernel(tc, xT, w, wp, gate, offs, pos1, pos2, out):
                     part[:, q, :], y[r][:].indirect(pos_sb[q][:, a // 16 : (a + n) // 16]), gate_sb[:, q, a : a + n], MULT
                 )
 
-        def turn_and_add(parts, n, tag="turn"):
-            bank = turns.tile([P, n // P, HALF], F32, tag=tag, name="turn")
+        def turn_and_add(parts, n, pool, name):
+            bank = pool.tile([P, n // P, HALF], F32, name=name)
             for i in range(2):
                 for b in range(n // P):
                     for q in range(2):
@@ -150,28 +169,29 @@ def tile_moe_nxt_lin_none_kernel(tc, xT, w, wp, gate, offs, pos1, pos2, out):
                         )
             return bank
 
-        c_rows = [keep.tile([P, n // P, 2, P, 2], BF16, name=f"c_rows{i}") for i, (a, n) in enumerate(GROUPS)]
+        c_rows = [keep.tile([P, n // P, 2, P, 2], BF16, name=f"c_rows{i}") for i, (a, n) in enumerate(GROUPS) if i > 0]
+        c_rows = [on_raw(1, 4, [P, 2, 2, P, 2], BF16, "c_rows0", skip=64)] + c_rows
 
         def round_c(i, h, bank, engine):
             engine(c_rows[i][:, :, :, 64 * h : 64 * (h + 1), :], bank.rearrange("t b (m u v) -> t b u m v", u=2, v=2))
 
-        gather_codes(0, "codes0")
-        gather_scales(0, "scales0")
+        gather_codes(0, keep.tile([P, 2 * C], U32, align_bytes=64, name="s_codes0"))
+        gather_scales(0, keep.tile([P, 2 * C], U8, align_bytes=64, name="s_scales0"))
         prepare_w(0, 0, nc.scalar.copy)
-        gather_codes(1, "w_raw0_0")
+        gather_codes(1, on_raw(0, 0, [P, 2 * C], U32, "s_codes1"))
         prepare_w(0, 1, nc.scalar.copy)
         experts(0, 0)
-        gather_scales(1, "w_raw0_1")
+        gather_scales(1, on_raw(0, 1, [P, 2 * C], U8, "s_scales1"))
         prepare_w(0, 2, nc.scalar.copy)
         prepare_w(0, 3, nc.scalar.copy)
-        gather_codes(2, "w_raw0_3")
+        gather_codes(2, on_raw(0, 3, [P, 2 * C], U32, "s_codes2"))
         experts(0, 1)
         prepare_w(0, 4, nc.scalar.copy)
-        gather_scales(2, "w_raw0_4")
+        gather_scales(2, on_raw(0, 4, [P, 2 * C], U8, "s_scales2", skip=64))
         prepare_w(0, 5, nc.scalar.copy)
         experts(0, 2)
         keep_results(0, (0, 1))
-        prepare_w(1, 0, nc.vector.tensor_copy, tag="w_raw0_5", bufs=1)
+        prepare_w(1, 0, nc.vector.tensor_copy, on_raw(0, 5, [P, HALF, PACK], BF16, "w_grp1_0"))
         prepare_w(1, 1, nc.scalar.copy)
         keep_results(0, (2,))
 
@@ -181,26 +201,26 @@ def tile_moe_nxt_lin_none_kernel(tc, xT, w, wp, gate, offs, pos1, pos2, out):
             gated(early[0, r], r, 0, 256)
         experts(1, 0)
         prepare_w(1, 2, nc.scalar.copy)
-        early[1, 0] = keep.tile([P, 2, 256], F32, align_bytes=64, tag="w_raw1_2", name="early1_0")
+        early[1, 0] = on_raw(1, 2, [P, 2, 256], F32, "early1_0")
         gated(early[1, 0], 0, 256, 256)
         prepare_w(1, 3, nc.scalar.copy)
         experts(1, 1)
-        early[1, 1] = keep.tile([P, 2, 256], F32, align_bytes=64, tag="w_raw1_3", name="early1_1")
+        early[1, 1] = on_raw(1, 3, [P, 2, 256], F32, "early1_1")
         gated(early[1, 1], 1, 256, 256)
         prepare_w(1, 4, nc.scalar.copy)
         prepare_w(1, 5, nc.scalar.copy)
         experts(1, 2)
-        last = keep.tile([P, 2, 2, 256], F32, align_bytes=64, tag="w_raw1_5", name="early2")
+        last = on_raw(1, 5, [P, 2, 2, 256], F32, "early2")
         for r in range(2):
             early[2, r] = last[:, r, :, :]
             gated(early[2, r], r, 512, 256)
-        keep_results(1, (0, 1, 2))
-
-        for s in range(2):
-            round_c(s, 0, turn_and_add([early[s, 0], early[s, 1]], 256)[:], nc.scalar.copy)
-        o, s = line_view(wp_grp[:], wp_raw[:])
-        nc.scalar.copy(o, s)
-        bank = turn_and_add([early[2, 0], early[2, 1]], 256)
+        keep_results(1, (0, 1))
+        round_c(0, 0, turn_and_add([early[0, 0], early[0, 1]], 256, turns, "first")[:], nc.scalar.copy)
+        nc.scalar.copy(*line_view(wp_grp[:, 0:HALF, :], wp_raw[:, :, 0:HALF]))
+        keep_results(1, (2,))
+        nc.scalar.copy(*line_view(wp_grp[:, HALF:M, :], wp_raw[:, :, HALF:M]))
+        round_c(1, 0, turn_and_add([early[1, 0], early[1, 1]], 256, banks, "bank")[:], nc.scalar.copy)
+        bank = turn_and_add([early[2, 0], early[2, 1]], 256, banks, "bank")
         round_c(2, 0, bank[:, 0:1, :], nc.scalar.copy)
         round_c(3, 0, bank[:, 1:2, :], nc.scalar.copy)
 
@@ -218,21 +238,23 @@ def tile_moe_nxt_lin_none_kernel(tc, xT, w, wp, gate, offs, pos1, pos2, out):
 
         def turn_back(i, engine):
             a, n = GROUPS[i]
-            round_c(i, 1, turn_and_add([late[i, 2], late[i, 3]], n)[:], engine)
+            round_c(i, 1, turn_and_add([late[i, 2], late[i, 3]], n, turns, "late")[:], engine)
             words = c_rows[i][:].rearrange("t b u p v -> t (b u p v)").bitcast(F32)
             bank = banks.tile([P, n // P, 2, P], F32, name="bank")
             for b in range(n // P):
                 for u in range(2):
                     nc.tensor.transpose(bank[:, b, u, :], words[:, (2 * b + u) * P : (2 * b + u + 1) * P], ident[:])
-            for b in range(n // P):
-                c_grp[i, b] = keep.tile([P, P * PACK], BF16, align_bytes=64, name=f"c_grp{i}_{b}")
-                engine(c_grp[i, b][:].bitcast(F32).rearrange("p (t u) -> p t u", u=2), bank[:, b, :, :].rearrange("p u t -> p t u"))
+            c_grp[i] = keep.tile([P, n * PACK], BF16, align_bytes=64, name=f"c_grp{i}")
+            engine(
+                c_grp[i][:].bitcast(F32).rearrange("p (b t u) -> p b t u", t=P, u=2),
+                bank[:].rearrange("p b u t -> p b t u"),
+            )
 
-        def project(i, engines):
+        o_banks = {}
+
+        def project(i):
             a, n = GROUPS[i]
-            for b in range(n // P):
-                cols = slice(b * P, (b + 1) * P)
-                nc.vector.quantize_mx(out=c_codes[i][:, cols].bitcast(FP8X4), scales=c_scales[i][:, cols], in_=c_grp[i, b][:])
+            nc.vector.quantize_mx(out=c_codes[i][:].bitcast(FP8X4), scales=c_scales[i][:], in_=c_grp[i][:])
             for half in range(2):
                 bank = banks.tile([P, 2, n], F32, name="bank")
                 for u in range(2):
@@ -246,27 +268,33 @@ def tile_moe_nxt_lin_none_kernel(tc, xT, w, wp, gate, offs, pos1, pos2, out):
                         start=True,
                         stop=True,
                     )
-                engines[half](o_sb[i][:, 2 * half : 2 * half + 2, :], bank[:])
+                o_banks[i, half] = bank
+
+        def store(i, engines):
+            a, n = GROUPS[i]
+            for half in range(2):
+                engines[half](o_sb[i][:, 2 * half : 2 * half + 2, :], o_banks[i, half][:])
             nc.sync.dma_start(out_view[:, :, a : a + n], o_sb[i][:])
 
-        for r in (2, 3):
-            combine(0, r, f"late0_{r}")
+        for i in range(2):
+            for r in (2, 3):
+                combine(i, r, f"late{i}_{r}")
         nc.vector.quantize_mx(
             out=wp_codes[:].bitcast(FP8X4), scales=wp_scales[:], in_=wp_grp[:].rearrange("p m j -> p (m j)")
         )
-        second = keep.tile([P, 2, 2, 256], F32, align_bytes=64, tag="wp_raw", name="late1")
-        for r in (2, 3):
-            late[1, r] = second[:, r - 2, :, :]
-            gated(late[1, r], r, 256, 256)
         turn_back(0, nc.scalar.copy)
-        project(0, (nc.scalar.copy, nc.scalar.copy))
-        both = keep.tile([P, 4, 2, P], F32, align_bytes=64, tag="c_grp0_0", name="late_both")
+        project(0)
+        both = keep.tile([P, 4, 2, P], F32, align_bytes=64, tag="c_grp0", name="late_both")
         for k, (i, r) in enumerate(((2, 2), (2, 3), (3, 2), (3, 3))):
             late[i, r] = both[:, k, :, :]
             gated(late[i, r], r, GROUPS[i][0], P)
         turn_back(1, nc.scalar.copy)
+        project(1)
         turn_back(2, nc.scalar.copy)
-        project(1, (nc.scalar.copy, nc.scalar.copy))
+        store(0, (nc.scalar.copy, nc.scalar.copy))
         turn_back(3, nc.vector.tensor_copy)
-        project(2, (nc.scalar.copy, nc.scalar.copy))
-        project(3, (nc.scalar.copy, nc.vector.tensor_copy))
+        store(1, (nc.scalar.copy, nc.scalar.copy))
+        project(2)
+        store(2, (nc.scalar.copy, nc.vector.tensor_copy))
+        project(3)
+        store(3, (nc.scalar.copy, nc.vector.tensor_copy))

@@ -16,6 +16,7 @@ U16 = mybir.dt.uint16
 U8 = mybir.dt.uint8
 FP8X4 = mybir.dt.float8_e4m3fn_x4
 MULT = mybir.AluOpType.mult
+ADD = mybir.AluOpType.add
 COPY = mybir.ActivationFunctionType.Copy
 
 FLOPS = 2 * SLOTS * K * N + 2 * T * N * M
@@ -23,9 +24,10 @@ BYTES = 4 * (K * T + E * K * N + N * M + 2 * T + M * T) + 2 * (SLOTS + 2 * T)
 
 RAW_BYTES = 4 * PACK * HALF
 Y_BYTES = 4 * SLOTS
-X_PIECE = 256
-X_VECTOR = 160
-GROUPS = ((0, 256), (256, 256), (512, 128), (640, 128))
+X_PIECES = ((0, 512, 344), (512, 256, 168))
+GP = 128
+Y_PIN = (3, 4)
+BLOCKS = T // P
 
 
 def tile_moe_nxt_lin_none_kernel(tc, xT, w, wp, gate, offs, pos1, pos2, out):
@@ -35,26 +37,25 @@ def tile_moe_nxt_lin_none_kernel(tc, xT, w, wp, gate, offs, pos1, pos2, out):
         keep = ctx.enter_context(tc.tile_pool(name="keep", bufs=1))
         placed = ctx.enter_context(tc.tile_pool(name="placed", bufs=1))
         banks = ctx.enter_context(tc.psum_pool(name="banks", bufs=6))
-        turns = ctx.enter_context(tc.psum_pool(name="turns", bufs=1))
+        turns = ctx.enter_context(tc.psum_pool(name="turns", bufs=2))
 
         offs_sb = lists.tile([P, SLOTS // 16], U16, name="offs_sb")
         pos_sb = [lists.tile([P, T // 16], U16, name=f"pos{q}_sb") for q in range(2)]
 
-        n_x = T // X_PIECE
         x_view = xT.rearrange("(p j) t -> p j t", j=PACK)
-        x_raw = [keep.tile([P, PACK, X_PIECE], F32, name=f"x_raw{i}") for i in range(n_x)]
-        x_grp = [keep.tile([P, X_PIECE, PACK], BF16, align_bytes=64, name=f"x_grp{i}") for i in range(n_x)]
+        x_raw = [keep.tile([P, PACK, n], F32, name=f"x_raw{i}") for i, (a, n, v) in enumerate(X_PIECES)]
+        x_grp = [keep.tile([P, n, PACK], BF16, align_bytes=64, name=f"x_grp{i}") for i, (a, n, v) in enumerate(X_PIECES)]
         x_codes = keep.tile([P, T], U32, align_bytes=64, name="x_codes")
         x_scales = keep.tile([P, T], U8, align_bytes=64, name="x_scales")
         raw_at, y_at, at = {}, {}, 0
         for h in range(2):
             for e in range(E):
-                if e == 4:
+                if e == Y_PIN[h]:
                     y_at[2 * h] = at
                     at = at + Y_BYTES - 64
                 raw_at[h, e] = at
                 at = at + RAW_BYTES
-                if e == 4:
+                if e == Y_PIN[h]:
                     y_at[2 * h + 1] = at - 64
                     at = at + Y_BYTES - 64
 
@@ -75,18 +76,21 @@ def tile_moe_nxt_lin_none_kernel(tc, xT, w, wp, gate, offs, pos1, pos2, out):
         def load_w(h, e):
             nc.sync.dma_start(w_raw[h][e][:], w[e].rearrange("(p j) n -> p j n", j=PACK)[:, :, h * HALF : (h + 1) * HALF])
 
-        for i in range(n_x):
-            nc.sync.dma_start(x_raw[i][:], x_view[:, :, i * X_PIECE : (i + 1) * X_PIECE])
+        for i, (a, n, v) in enumerate(X_PIECES):
+            nc.sync.dma_start(x_raw[i][:], x_view[:, :, a : a + n])
         nc.sync.dma_start(offs_sb[:], offs)
-        for e in range(E):
-            load_w(0, e)
-        load_w(1, 0)
-        load_w(1, 1)
         nc.sync.dma_start(pos_sb[0][:], pos1)
         nc.sync.dma_start(pos_sb[1][:], pos2)
-        nc.sync.dma_start(gate_sb[:], gate[:, 0:P, :].rearrange("g p t -> p g t"))
+        for e in range(E):
+            load_w(0, e)
+        gate_view = gate[:, 0:P, :].rearrange("g p t -> p g t")
+        load_w(1, 0)
+        nc.sync.dma_start(gate_sb[:, :, 0:256], gate_view[:, :, 0:256])
+        load_w(1, 1)
+        nc.sync.dma_start(gate_sb[:, :, 256:512], gate_view[:, :, 256:512])
         for e in range(2, E):
             load_w(1, e)
+        nc.sync.dma_start(gate_sb[:, :, 512:T], gate_view[:, :, 512:T])
         nc.sync.dma_start(wp_raw[:], wp.rearrange("(p j) m -> p j m", j=PACK))
 
         nc.gpsimd.memset(x_scales[:], 0)
@@ -95,14 +99,14 @@ def tile_moe_nxt_lin_none_kernel(tc, xT, w, wp, gate, offs, pos1, pos2, out):
         def line_view(grouped, raw):
             return (grouped.rearrange("p (c i) j -> p c j i", i=4), raw.rearrange("p j (c i) -> p c j i", i=4))
 
-        for i in range(n_x):
-            o, s = line_view(x_grp[i][:, 0:X_VECTOR, :], x_raw[i][:, :, 0:X_VECTOR])
+        for i, (a, n, v) in enumerate(X_PIECES):
+            o, s = line_view(x_grp[i][:, 0:v, :], x_raw[i][:, :, 0:v])
             nc.vector.tensor_copy(o, s)
-            o, s = line_view(x_grp[i][:, X_VECTOR:X_PIECE, :], x_raw[i][:, :, X_VECTOR:X_PIECE])
+            o, s = line_view(x_grp[i][:, v:n, :], x_raw[i][:, :, v:n])
             nc.scalar.activation(o, s, COPY)
             nc.vector.quantize_mx(
-                out=x_codes[:, i * X_PIECE : (i + 1) * X_PIECE].bitcast(FP8X4),
-                scales=x_scales[:, i * X_PIECE : (i + 1) * X_PIECE],
+                out=x_codes[:, a : a + n].bitcast(FP8X4),
+                scales=x_scales[:, a : a + n],
                 in_=x_grp[i][:].rearrange("p t j -> p (t j)"),
             )
 
@@ -116,11 +120,14 @@ def tile_moe_nxt_lin_none_kernel(tc, xT, w, wp, gate, offs, pos1, pos2, out):
             s_scales[g] = tile
             nc.vector.tensor_copy(s_scales[g][:], x_scales[:].indirect(offs_sb[:, g * 32 : (g + 1) * 32]))
 
-        def prepare_w(h, e, engine, grouped=None):
+        def prepare_w(h, e, engine, grouped=None, share=0):
             if grouped is None:
-                grouped = keep.tile([P, HALF, PACK], BF16, align_bytes=64, tag="w_grp", bufs=4, name=f"w_grp{h}_{e}")
-            o, s = line_view(grouped[:], w_raw[h][e][:])
-            engine(o, s)
+                grouped = keep.tile([P, HALF, PACK], BF16, align_bytes=64, tag=f"w_grp{h}", bufs=2 + 2 * h, name=f"w_grp{h}_{e}")
+            engine(*line_view(grouped[:, share:HALF, :], w_raw[h][e][:, :, share:HALF]))
+            if share > 0:
+                nc.gpsimd.tensor_scalar(
+                    grouped[:, 0:share, :], w_raw[h][e][:, :, 0:share].rearrange("p j n -> p n j"), 1.0, 0.0, MULT, ADD
+                )
             nc.vector.quantize_mx(
                 out=w_codes[h][e][:].bitcast(FP8X4), scales=w_scales[h][e][:], in_=grouped[:].rearrange("p n j -> p (n j)")
             )
@@ -143,10 +150,9 @@ def tile_moe_nxt_lin_none_kernel(tc, xT, w, wp, gate, offs, pos1, pos2, out):
                         stop=True,
                     )
 
-        def keep_results(h, pairs):
+        def keep_results(r, pairs):
             for g in pairs:
-                for r in (2 * h, 2 * h + 1):
-                    nc.scalar.copy(y[r][:, 2 * g * C : 2 * (g + 1) * C], y_banks[r, g][:])
+                nc.scalar.copy(y[r][:, 2 * g * C : 2 * (g + 1) * C], y_banks[r, g][:])
 
         def gated(part, r, a, n):
             for q in range(2):
@@ -169,132 +175,151 @@ def tile_moe_nxt_lin_none_kernel(tc, xT, w, wp, gate, offs, pos1, pos2, out):
                         )
             return bank
 
-        c_rows = [keep.tile([P, n // P, 2, P, 2], BF16, name=f"c_rows{i}") for i, (a, n) in enumerate(GROUPS) if i > 0]
-        c_rows = [on_raw(1, 4, [P, 2, 2, P, 2], BF16, "c_rows0", skip=64)] + c_rows
+        c_rows = [on_raw(1, 4, [P, 2, P, 2], BF16, f"c_rows{b}", skip=64 + 1024 * b) for b in range(2)]
+        c_rows = c_rows + [keep.tile([P, 2, P, 2], BF16, align_bytes=64, name=f"c_rows{b}") for b in range(2, BLOCKS)]
 
         def round_c(i, h, bank, engine):
-            engine(c_rows[i][:, :, :, 64 * h : 64 * (h + 1), :], bank.rearrange("t b (m u v) -> t b u m v", u=2, v=2))
+            engine(c_rows[i][:, :, 64 * h : 64 * (h + 1), :], bank.rearrange("t (m u v) -> t u m v", u=2, v=2))
 
         gather_codes(0, keep.tile([P, 2 * C], U32, align_bytes=64, name="s_codes0"))
         gather_scales(0, keep.tile([P, 2 * C], U8, align_bytes=64, name="s_scales0"))
-        prepare_w(0, 0, nc.scalar.copy)
+        prepare_w(0, 0, nc.scalar.copy, share=GP)
         gather_codes(1, on_raw(0, 0, [P, 2 * C], U32, "s_codes1"))
-        prepare_w(0, 1, nc.scalar.copy)
+        prepare_w(0, 1, nc.scalar.copy, share=GP)
         experts(0, 0)
         gather_scales(1, on_raw(0, 1, [P, 2 * C], U8, "s_scales1"))
-        prepare_w(0, 2, nc.scalar.copy)
-        prepare_w(0, 3, nc.scalar.copy)
-        gather_codes(2, on_raw(0, 3, [P, 2 * C], U32, "s_codes2"))
+        prepare_w(0, 2, nc.scalar.copy, share=GP)
+        gather_codes(2, on_raw(0, 2, [P, 2 * C], U32, "s_codes2"))
+        prepare_w(0, 3, nc.scalar.copy, share=GP)
+        gather_scales(2, on_raw(0, 3, [P, 2 * C], U8, "s_scales2", skip=64))
         experts(0, 1)
-        prepare_w(0, 4, nc.scalar.copy)
-        gather_scales(2, on_raw(0, 4, [P, 2 * C], U8, "s_scales2", skip=64))
-        prepare_w(0, 5, nc.scalar.copy)
+        prepare_w(0, 4, nc.scalar.copy, share=GP)
+        prepare_w(0, 5, nc.scalar.copy, share=GP)
         experts(0, 2)
-        keep_results(0, (0, 1))
+        keep_results(0, (0,))
+        keep_results(1, (0,))
+        keep_results(0, (1, 2))
+        keep_results(1, (1, 2))
         prepare_w(1, 0, nc.vector.tensor_copy, on_raw(0, 5, [P, HALF, PACK], BF16, "w_grp1_0"))
-        prepare_w(1, 1, nc.scalar.copy)
-        keep_results(0, (2,))
 
         early = {}
         for r in range(2):
             early[0, r] = keep.tile([P, 2, 256], F32, name=f"early0_{r}")
             gated(early[0, r], r, 0, 256)
-        experts(1, 0)
-        prepare_w(1, 2, nc.scalar.copy)
-        early[1, 0] = on_raw(1, 2, [P, 2, 256], F32, "early1_0")
-        gated(early[1, 0], 0, 256, 256)
-        prepare_w(1, 3, nc.scalar.copy)
-        experts(1, 1)
-        early[1, 1] = on_raw(1, 3, [P, 2, 256], F32, "early1_1")
-        gated(early[1, 1], 1, 256, 256)
-        prepare_w(1, 4, nc.scalar.copy)
-        prepare_w(1, 5, nc.scalar.copy)
-        experts(1, 2)
-        last = on_raw(1, 5, [P, 2, 2, 256], F32, "early2")
+        for e in range(1, E):
+            prepare_w(1, e, nc.scalar.copy)
+            if e % 2 == 1:
+                experts(1, e // 2)
+            if e < 3:
+                early[1, e - 1] = on_raw(1, e, [P, 2, 256], F32, f"early1_{e - 1}")
+                gated(early[1, e - 1], e - 1, 256, 256)
         for r in range(2):
-            early[2, r] = last[:, r, :, :]
+            early[2, r] = on_raw(1, 5, [P, 2, 256], F32, f"early2_{r}", skip=2048 * r)
             gated(early[2, r], r, 512, 256)
-        keep_results(1, (0, 1))
-        round_c(0, 0, turn_and_add([early[0, 0], early[0, 1]], 256, turns, "first")[:], nc.scalar.copy)
-        nc.scalar.copy(*line_view(wp_grp[:, 0:HALF, :], wp_raw[:, :, 0:HALF]))
-        keep_results(1, (2,))
-        nc.scalar.copy(*line_view(wp_grp[:, HALF:M, :], wp_raw[:, :, HALF:M]))
-        round_c(1, 0, turn_and_add([early[1, 0], early[1, 1]], 256, banks, "bank")[:], nc.scalar.copy)
-        bank = turn_and_add([early[2, 0], early[2, 1]], 256, banks, "bank")
-        round_c(2, 0, bank[:, 0:1, :], nc.scalar.copy)
-        round_c(3, 0, bank[:, 1:2, :], nc.scalar.copy)
+        keep_results(2, (0, 1))
+        keep_results(3, (0, 1))
+        keep_results(2, (2,))
+        keep_results(3, (2,))
+        early_banks = [turn_and_add([early[0, 0], early[0, 1]], 256, turns, "late")]
+        early_banks = early_banks + [turn_and_add([early[s, 0], early[s, 1]], 256, banks, "bank") for s in (1, 2)]
 
-        c_codes = [keep.tile([P, n], U32, align_bytes=64, name=f"c_codes{i}") for i, (a, n) in enumerate(GROUPS)]
-        c_scales = [keep.tile([P, n], U8, align_bytes=64, name=f"c_scales{i}") for i, (a, n) in enumerate(GROUPS)]
-        o_sb = [keep.tile([P, 4, n], F32, name=f"o_sb{i}") for i, (a, n) in enumerate(GROUPS)]
+        c_grp = [keep.tile([P, P * PACK], BF16, align_bytes=64, name=f"c_grp{b}") for b in range(BLOCKS)]
+        c_codes = [keep.tile([P, P], U32, align_bytes=64, name=f"c_codes{b}") for b in range(BLOCKS)]
+        c_scales = [keep.tile([P, P], U8, align_bytes=64, name=f"c_scales{b}") for b in range(BLOCKS)]
+        o_sb = [keep.tile([P, 4, 2 * P], F32, name=f"o_sb{s}") for s in range(BLOCKS // 2)]
         out_view = out.rearrange("(f p) t -> p f t", p=P)
-        late = {}
-        c_grp = {}
+        late, o_banks = {}, {}
 
-        def combine(i, r, tag):
-            a, n = GROUPS[i]
-            late[i, r] = keep.tile([P, 2, n], F32, align_bytes=64, tag=tag, name=f"late{i}_{r}")
-            gated(late[i, r], r, a, n)
+        def round_early(b):
+            round_c(b, 0, early_banks[b // 2][:, b % 2, :], nc.scalar.copy)
 
-        def turn_back(i, engine):
-            a, n = GROUPS[i]
-            round_c(i, 1, turn_and_add([late[i, 2], late[i, 3]], n, turns, "late")[:], engine)
-            words = c_rows[i][:].rearrange("t b u p v -> t (b u p v)").bitcast(F32)
-            bank = banks.tile([P, n // P, 2, P], F32, name="bank")
-            for b in range(n // P):
-                for u in range(2):
-                    nc.tensor.transpose(bank[:, b, u, :], words[:, (2 * b + u) * P : (2 * b + u + 1) * P], ident[:])
-            c_grp[i] = keep.tile([P, n * PACK], BF16, align_bytes=64, name=f"c_grp{i}")
-            engine(
-                c_grp[i][:].bitcast(F32).rearrange("p (b t u) -> p b t u", t=P, u=2),
-                bank[:].rearrange("p b u t -> p b t u"),
-            )
+        def interleave_wp(h):
+            nc.scalar.copy(*line_view(wp_grp[:, h * HALF : (h + 1) * HALF, :], wp_raw[:, :, h * HALF : (h + 1) * HALF]))
 
-        o_banks = {}
+        def combine(b, tag):
+            late[b] = keep.tile([P, 2, 2, P], F32, align_bytes=64, tag=tag, name=f"late{b}")
+            for i in range(2):
+                gated(late[b][:, i, :, :], 2 + i, b * P, P)
 
-        def project(i):
-            a, n = GROUPS[i]
-            nc.vector.quantize_mx(out=c_codes[i][:].bitcast(FP8X4), scales=c_scales[i][:], in_=c_grp[i][:])
+        def round_late(b, engine):
+            round_c(b, 1, turn_and_add([late[b][:, 0, :, :], late[b][:, 1, :, :]], P, turns, "late")[:, 0, :], engine)
+
+        def turn_back(b, engine):
+            words = c_rows[b][:].rearrange("t u p v -> t (u p v)").bitcast(F32)
+            bank = banks.tile([P, 2, P], F32, name="bank")
+            for u in range(2):
+                nc.tensor.transpose(bank[:, u, :], words[:, u * P : (u + 1) * P], ident[:])
+            engine(c_grp[b][:].bitcast(F32).rearrange("p (t u) -> p t u", u=2), bank[:].rearrange("p u t -> p t u"))
+
+        def project(b):
+            nc.vector.quantize_mx(out=c_codes[b][:].bitcast(FP8X4), scales=c_scales[b][:], in_=c_grp[b][:])
             for half in range(2):
-                bank = banks.tile([P, 2, n], F32, name="bank")
+                o_banks[b, half] = banks.tile([P, 2, P], F32, name="bank")
                 for u in range(2):
                     f = 2 * half + u
                     nc.tensor.matmul_mx(
-                        out=bank[:, u, :],
+                        out=o_banks[b, half][:, u, :],
                         lhsT=wp_codes[:, f * P : (f + 1) * P].bitcast(FP8X4),
                         lhsT_scale=wp_scales[:, f * P : (f + 1) * P],
-                        rhs=c_codes[i][:].bitcast(FP8X4),
-                        rhs_scale=c_scales[i][:],
+                        rhs=c_codes[b][:].bitcast(FP8X4),
+                        rhs_scale=c_scales[b][:],
                         start=True,
                         stop=True,
                     )
-                o_banks[i, half] = bank
 
-        def store(i, engines):
-            a, n = GROUPS[i]
+        def store(b, engines):
+            cols = slice(b % 2 * P, (b % 2 + 1) * P)
             for half in range(2):
-                engines[half](o_sb[i][:, 2 * half : 2 * half + 2, :], o_banks[i, half][:])
-            nc.sync.dma_start(out_view[:, :, a : a + n], o_sb[i][:])
+                rows = slice(2 * half, 2 * (half + 1))
+                engines[half](o_sb[b // 2][:, rows, cols], o_banks[b, half][:])
+                if b == BLOCKS - 1:
+                    nc.sync.dma_start(out_view[:, rows, b * P : (b + 1) * P], o_sb[b // 2][:, rows, cols])
+            if b == BLOCKS - 2:
+                nc.sync.dma_start(out_view[:, :, b * P : (b + 1) * P], o_sb[b // 2][:, :, cols])
+            elif b % 2 == 1 and b < BLOCKS - 1:
+                nc.sync.dma_start(out_view[:, :, (b - 1) * P : (b + 1) * P], o_sb[b // 2][:])
 
-        for i in range(2):
-            for r in (2, 3):
-                combine(i, r, f"late{i}_{r}")
-        nc.vector.quantize_mx(
-            out=wp_codes[:].bitcast(FP8X4), scales=wp_scales[:], in_=wp_grp[:].rearrange("p m j -> p (m j)")
-        )
+        def quantise_wp():
+            nc.vector.quantize_mx(
+                out=wp_codes[:].bitcast(FP8X4), scales=wp_scales[:], in_=wp_grp[:].rearrange("p m j -> p (m j)")
+            )
+
+        combine(0, "late0")
+        combine(1, "late1")
+        combine(2, "late2")
+        round_early(0)
+        round_early(1)
+        interleave_wp(0)
+        round_late(0, nc.scalar.copy)
         turn_back(0, nc.scalar.copy)
-        project(0)
-        both = keep.tile([P, 4, 2, P], F32, align_bytes=64, tag="c_grp0", name="late_both")
-        for k, (i, r) in enumerate(((2, 2), (2, 3), (3, 2), (3, 3))):
-            late[i, r] = both[:, k, :, :]
-            gated(late[i, r], r, GROUPS[i][0], P)
+        interleave_wp(1)
+        quantise_wp()
+        round_late(1, nc.scalar.copy)
+        round_early(2)
+        round_early(3)
         turn_back(1, nc.scalar.copy)
-        project(1)
+        project(0)
+        combine(3, "c_grp0")
+        round_late(2, nc.scalar.copy)
         turn_back(2, nc.scalar.copy)
+        round_early(4)
+        round_early(5)
+        project(1)
+        combine(4, "c_grp1")
+        round_late(3, nc.scalar.copy)
+        turn_back(3, nc.scalar.copy)
         store(0, (nc.scalar.copy, nc.scalar.copy))
-        turn_back(3, nc.vector.tensor_copy)
-        store(1, (nc.scalar.copy, nc.scalar.copy))
         project(2)
-        store(2, (nc.scalar.copy, nc.vector.tensor_copy))
+        combine(5, "c_grp2")
+        round_late(4, nc.scalar.copy)
+        turn_back(4, nc.scalar.copy)
+        store(1, (nc.scalar.copy, nc.scalar.copy))
+        store(2, (nc.scalar.copy, nc.scalar.copy))
         project(3)
-        store(3, (nc.scalar.copy, nc.vector.tensor_copy))
+        round_late(5, nc.vector.tensor_copy)
+        store(3, (nc.scalar.copy, nc.scalar.copy))
+        turn_back(5, nc.vector.tensor_copy)
+        project(4)
+        project(5)
+        store(4, (nc.scalar.copy, nc.scalar.copy))
+        store(5, (nc.scalar.copy, nc.vector.tensor_copy))

@@ -16,7 +16,6 @@ U16 = mybir.dt.uint16
 U8 = mybir.dt.uint8
 FP8X4 = mybir.dt.float8_e4m3fn_x4
 MULT = mybir.AluOpType.mult
-ADD = mybir.AluOpType.add
 COPY = mybir.ActivationFunctionType.Copy
 
 FLOPS = 2 * SLOTS * K * N + 2 * T * N * M
@@ -25,9 +24,12 @@ BYTES = 4 * (K * T + E * K * N + N * M + 2 * T + M * T) + 2 * (SLOTS + 2 * T)
 RAW_BYTES = 4 * PACK * HALF
 Y_BYTES = 4 * SLOTS
 X_PIECES = ((0, 512, 344), (512, 256, 168))
-GP = 128
-Y_PIN = (3, 4)
-BLOCKS = T // P
+Y_PIN = (5, 4)
+Y_BANK = ((0, 1, 2), (3, 4, 5), (6, 7, 0), (1, 2, 3))
+WINDOW = 1024
+TRIO = 3 * C
+GROUPS = ((0, 384), (384, 256), (640, 128))
+UNITS = ((0, 256), (256, 128), (384, 256), (640, 128))
 
 
 def tile_moe_nxt_lin_none_kernel(tc, xT, w, wp, gate, offs, pos1, pos2, out):
@@ -36,8 +38,7 @@ def tile_moe_nxt_lin_none_kernel(tc, xT, w, wp, gate, offs, pos1, pos2, out):
         lists = ctx.enter_context(tc.tile_pool(name="lists", bufs=1))
         keep = ctx.enter_context(tc.tile_pool(name="keep", bufs=1))
         placed = ctx.enter_context(tc.tile_pool(name="placed", bufs=1))
-        banks = ctx.enter_context(tc.psum_pool(name="banks", bufs=6))
-        turns = ctx.enter_context(tc.psum_pool(name="turns", bufs=2))
+        banks = ctx.enter_context(tc.psum_pool(name="banks", bufs=1))
 
         offs_sb = lists.tile([P, SLOTS // 16], U16, name="offs_sb")
         pos_sb = [lists.tile([P, T // 16], U16, name=f"pos{q}_sb") for q in range(2)]
@@ -45,8 +46,8 @@ def tile_moe_nxt_lin_none_kernel(tc, xT, w, wp, gate, offs, pos1, pos2, out):
         x_view = xT.rearrange("(p j) t -> p j t", j=PACK)
         x_raw = [keep.tile([P, PACK, n], F32, name=f"x_raw{i}") for i, (a, n, v) in enumerate(X_PIECES)]
         x_grp = [keep.tile([P, n, PACK], BF16, align_bytes=64, name=f"x_grp{i}") for i, (a, n, v) in enumerate(X_PIECES)]
-        x_codes = keep.tile([P, T], U32, align_bytes=64, name="x_codes")
-        x_scales = keep.tile([P, T], U8, align_bytes=64, name="x_scales")
+        x_codes = keep.tile([P, WINDOW], U32, align_bytes=64, name="x_codes")
+        x_scales = keep.tile([P, WINDOW], U8, align_bytes=64, name="x_scales")
         raw_at, y_at, at = {}, {}, 0
         for h in range(2):
             for e in range(E):
@@ -85,15 +86,17 @@ def tile_moe_nxt_lin_none_kernel(tc, xT, w, wp, gate, offs, pos1, pos2, out):
             load_w(0, e)
         gate_view = gate[:, 0:P, :].rearrange("g p t -> p g t")
         load_w(1, 0)
-        nc.sync.dma_start(gate_sb[:, :, 0:256], gate_view[:, :, 0:256])
         load_w(1, 1)
-        nc.sync.dma_start(gate_sb[:, :, 256:512], gate_view[:, :, 256:512])
-        for e in range(2, E):
-            load_w(1, e)
-        nc.sync.dma_start(gate_sb[:, :, 512:T], gate_view[:, :, 512:T])
+        load_w(1, 2)
+        load_w(1, 3)
+        nc.sync.dma_start(gate_sb[:, 0, :], gate_view[:, 0, :])
+        load_w(1, 4)
+        nc.sync.dma_start(gate_sb[:, 1, :], gate_view[:, 1, :])
+        load_w(1, 5)
         nc.sync.dma_start(wp_raw[:], wp.rearrange("(p j) m -> p j m", j=PACK))
 
         nc.gpsimd.memset(x_scales[:], 0)
+        nc.gpsimd.memset(x_codes[:, T:WINDOW], 0)
         make_identity(nc, ident[:])
 
         def line_view(grouped, raw):
@@ -114,212 +117,179 @@ def tile_moe_nxt_lin_none_kernel(tc, xT, w, wp, gate, offs, pos1, pos2, out):
 
         def gather_codes(g, tile):
             s_codes[g] = tile
-            nc.vector.tensor_copy(s_codes[g][:], x_codes[:].indirect(offs_sb[:, g * 32 : (g + 1) * 32]))
+            nc.vector.tensor_copy(s_codes[g][:], x_codes[:].indirect(offs_sb[:, g * TRIO // 16 : (g + 1) * TRIO // 16]))
 
         def gather_scales(g, tile):
             s_scales[g] = tile
-            nc.vector.tensor_copy(s_scales[g][:], x_scales[:].indirect(offs_sb[:, g * 32 : (g + 1) * 32]))
+            nc.vector.tensor_copy(s_scales[g][:], x_scales[:].indirect(offs_sb[:, g * TRIO // 16 : (g + 1) * TRIO // 16]))
 
-        def prepare_w(h, e, engine, grouped=None, share=0):
-            if grouped is None:
-                grouped = keep.tile([P, HALF, PACK], BF16, align_bytes=64, tag=f"w_grp{h}", bufs=2 + 2 * h, name=f"w_grp{h}_{e}")
-            engine(*line_view(grouped[:, share:HALF, :], w_raw[h][e][:, :, share:HALF]))
-            if share > 0:
-                nc.gpsimd.tensor_scalar(
-                    grouped[:, 0:share, :], w_raw[h][e][:, :, 0:share].rearrange("p j n -> p n j"), 1.0, 0.0, MULT, ADD
-                )
+        def on_vector(grouped, raw):
+            nc.vector.tensor_copy(*line_view(grouped, raw))
+
+        def on_scalar(grouped, raw):
+            nc.scalar.copy(*line_view(grouped, raw))
+
+        def prepare_w(h, e, interleave, tag):
+            grouped = keep.tile([P, HALF, PACK], BF16, align_bytes=64, tag=tag, name=f"w_grp{h}_{e}")
+            interleave(grouped[:], w_raw[h][e][:])
             nc.vector.quantize_mx(
                 out=w_codes[h][e][:].bitcast(FP8X4), scales=w_scales[h][e][:], in_=grouped[:].rearrange("p n j -> p (n j)")
             )
 
         y_banks = {}
 
-        def experts(h, g):
-            for i in range(2):
-                bank = banks.tile([P, 2 * C], F32, name="bank")
-                y_banks[2 * h + i, g] = bank
-                for half in range(2):
-                    e = 2 * g + half
-                    nc.tensor.matmul_mx(
-                        out=bank[:, half * C : (half + 1) * C],
-                        lhsT=w_codes[h][e][:, i * P : (i + 1) * P].bitcast(FP8X4),
-                        lhsT_scale=w_scales[h][e][:, i * P : (i + 1) * P],
-                        rhs=s_codes[g][:, half * C : (half + 1) * C].bitcast(FP8X4),
-                        rhs_scale=s_scales[g][:, half * C : (half + 1) * C],
-                        start=True,
-                        stop=True,
-                    )
-
-        def keep_results(r, pairs):
-            for g in pairs:
-                nc.scalar.copy(y[r][:, 2 * g * C : 2 * (g + 1) * C], y_banks[r, g][:])
-
-        def gated(part, r, a, n):
-            for q in range(2):
-                nc.vector.tensor_tensor(
-                    part[:, q, :], y[r][:].indirect(pos_sb[q][:, a // 16 : (a + n) // 16]), gate_sb[:, q, a : a + n], MULT
+        def experts(r, g):
+            h, i = divmod(r, 2)
+            y_banks[r, g] = banks.tile([P, 2 * C], F32, name=f"bank{Y_BANK[r][g]}")
+            for half in range(2):
+                e = 2 * g + half
+                nc.tensor.matmul_mx(
+                    out=y_banks[r, g][:, half * C : (half + 1) * C],
+                    lhsT=w_codes[h][e][:, i * P : (i + 1) * P].bitcast(FP8X4),
+                    lhsT_scale=w_scales[h][e][:, i * P : (i + 1) * P],
+                    rhs=s_codes[e // 3][:, e % 3 * C : (e % 3 + 1) * C].bitcast(FP8X4),
+                    rhs_scale=s_scales[e // 3][:, e % 3 * C : (e % 3 + 1) * C],
+                    start=True,
+                    stop=True,
                 )
 
-        def turn_and_add(parts, n, pool, name):
-            bank = pool.tile([P, n // P, HALF], F32, name=name)
-            for i in range(2):
-                for b in range(n // P):
-                    for q in range(2):
-                        nc.tensor.matmul(
-                            bank[:, b, i * P : (i + 1) * P],
-                            parts[i][:, q, b * P : (b + 1) * P],
-                            ident[:],
-                            start=(q == 0),
-                            stop=(q == 1),
-                            is_transpose=True,
-                        )
-            return bank
+        def keep_result(r, g, engine=nc.scalar.copy):
+            engine(y[r][:, 2 * g * C : 2 * (g + 1) * C], y_banks[r, g][:])
 
-        c_rows = [on_raw(1, 4, [P, 2, P, 2], BF16, f"c_rows{b}", skip=64 + 1024 * b) for b in range(2)]
-        c_rows = c_rows + [keep.tile([P, 2, P, 2], BF16, align_bytes=64, name=f"c_rows{b}") for b in range(2, BLOCKS)]
+        def gated(part, q, r, a, n):
+            nc.vector.tensor_tensor(
+                part, y[r][:].indirect(pos_sb[q][:, a // 16 : (a + n) // 16]), gate_sb[:, q, a : a + n], MULT
+            )
 
-        def round_c(i, h, bank, engine):
-            engine(c_rows[i][:, :, 64 * h : 64 * (h + 1), :], bank.rearrange("t (m u v) -> t u m v", u=2, v=2))
+        def add_turned(bank, i, parts, n):
+            for b in range(n // P):
+                for q in range(2):
+                    nc.tensor.matmul(
+                        bank[:, b, i * P : (i + 1) * P],
+                        parts[q][:, b * P : (b + 1) * P],
+                        ident[:],
+                        start=(q == 0),
+                        stop=(q == 1),
+                        is_transpose=True,
+                    )
 
-        gather_codes(0, keep.tile([P, 2 * C], U32, align_bytes=64, name="s_codes0"))
-        gather_scales(0, keep.tile([P, 2 * C], U8, align_bytes=64, name="s_scales0"))
-        prepare_w(0, 0, nc.scalar.copy, share=GP)
-        gather_codes(1, on_raw(0, 0, [P, 2 * C], U32, "s_codes1"))
-        prepare_w(0, 1, nc.scalar.copy, share=GP)
-        experts(0, 0)
-        gather_scales(1, on_raw(0, 1, [P, 2 * C], U8, "s_scales1"))
-        prepare_w(0, 2, nc.scalar.copy, share=GP)
-        gather_codes(2, on_raw(0, 2, [P, 2 * C], U32, "s_codes2"))
-        prepare_w(0, 3, nc.scalar.copy, share=GP)
-        gather_scales(2, on_raw(0, 3, [P, 2 * C], U8, "s_scales2", skip=64))
-        experts(0, 1)
-        prepare_w(0, 4, nc.scalar.copy, share=GP)
-        prepare_w(0, 5, nc.scalar.copy, share=GP)
-        experts(0, 2)
-        keep_results(0, (0,))
-        keep_results(1, (0,))
-        keep_results(0, (1, 2))
-        keep_results(1, (1, 2))
-        prepare_w(1, 0, nc.vector.tensor_copy, on_raw(0, 5, [P, HALF, PACK], BF16, "w_grp1_0"))
+        c_rows = [keep.tile([P, n // P, 2, P, 2], BF16, align_bytes=64, name=f"c_rows{u}") for u, (a, n) in enumerate(UNITS)]
+
+        def round_c(u, h, bank, engine):
+            engine(c_rows[u][:, :, :, 64 * h : 64 * (h + 1), :], bank[:].rearrange("t b (m w v) -> t b w m v", w=2, v=2))
+
+        gather_codes(0, keep.tile([P, TRIO], U32, align_bytes=64, name="s_codes0"))
+        gather_scales(0, keep.tile([P, TRIO], U8, align_bytes=64, name="s_scales0"))
+        prepare_w(0, 0, on_scalar, "g0")
+        prepare_w(0, 1, on_scalar, "g1")
+        prepare_w(0, 2, on_scalar, "g2")
+        gather_codes(1, on_raw(0, 2, [P, TRIO], U32, "s_codes1"))
+        prepare_w(0, 3, on_scalar, "g3")
+        prepare_w(0, 4, on_scalar, "g4")
+        prepare_w(0, 5, on_scalar, "g5")
+        gather_scales(1, on_raw(0, 5, [P, TRIO], U8, "s_scales1", skip=64))
+        for r in range(2):
+            experts(r, 0)
+            keep_result(r, 0)
+        for r in range(2):
+            experts(r, 1)
+            experts(r, 2)
+        prepare_w(1, 0, on_scalar, "g0")
+        prepare_w(1, 1, on_scalar, "g1")
+        prepare_w(1, 2, on_scalar, "g2")
+        prepare_w(1, 3, on_vector, "w_last")
+        keep_result(0, 1)
+        keep_result(0, 2, nc.scalar.copy)
+        keep_result(1, 1)
+        keep_result(1, 2)
 
         early = {}
+        early[0, 0] = keep.tile([P, T], F32, align_bytes=64, name="early0_0")
+        gated(early[0, 0][:], 0, 0, 0, T)
+        early[0, 1] = keep.tile([P, T], F32, align_bytes=64, name="early0_1")
+        gated(early[0, 1][:], 1, 0, 0, T)
+        prepare_w(1, 4, on_scalar, "g4")
+        prepare_w(1, 5, on_scalar, "g5")
+        early[1, 0] = on_raw(1, 5, [P, T], F32, "early1_0")
+        gated(early[1, 0][:], 0, 1, 0, T)
+        early[1, 1] = on_raw(1, 5, [P, T], F32, "early1_1", skip=4 * T)
+        gated(early[1, 1][:], 1, 1, 0, T)
+        for g in range(3):
+            for r in (2, 3):
+                experts(r, g)
+        for g in range(3):
+            for r in (2, 3):
+                keep_result(r, g)
+        nc.scalar.copy(*line_view(wp_grp[:], wp_raw[:]))
+        early_banks = [banks.tile([P, n // P, HALF], F32, name=f"bank{4 + u}") for u, (a, n) in enumerate(UNITS)]
         for r in range(2):
-            early[0, r] = keep.tile([P, 2, 256], F32, name=f"early0_{r}")
-            gated(early[0, r], r, 0, 256)
-        for e in range(1, E):
-            prepare_w(1, e, nc.scalar.copy)
-            if e % 2 == 1:
-                experts(1, e // 2)
-            if e < 3:
-                early[1, e - 1] = on_raw(1, e, [P, 2, 256], F32, f"early1_{e - 1}")
-                gated(early[1, e - 1], e - 1, 256, 256)
-        for r in range(2):
-            early[2, r] = on_raw(1, 5, [P, 2, 256], F32, f"early2_{r}", skip=2048 * r)
-            gated(early[2, r], r, 512, 256)
-        keep_results(2, (0, 1))
-        keep_results(3, (0, 1))
-        keep_results(2, (2,))
-        keep_results(3, (2,))
-        early_banks = [turn_and_add([early[0, 0], early[0, 1]], 256, turns, "late")]
-        early_banks = early_banks + [turn_and_add([early[s, 0], early[s, 1]], 256, banks, "bank") for s in (1, 2)]
+            for u, (a, n) in enumerate(UNITS):
+                add_turned(early_banks[u], r, [early[r, q][:, a : a + n] for q in range(2)], n)
+        for u in range(len(UNITS)):
+            round_c(u, 0, early_banks[u], nc.scalar.copy)
 
-        c_grp = [keep.tile([P, P * PACK], BF16, align_bytes=64, name=f"c_grp{b}") for b in range(BLOCKS)]
-        c_codes = [keep.tile([P, P], U32, align_bytes=64, name=f"c_codes{b}") for b in range(BLOCKS)]
-        c_scales = [keep.tile([P, P], U8, align_bytes=64, name=f"c_scales{b}") for b in range(BLOCKS)]
-        o_sb = [keep.tile([P, 4, 2 * P], F32, name=f"o_sb{s}") for s in range(BLOCKS // 2)]
+        c_grp = [keep.tile([P, n * PACK], BF16, align_bytes=64, name=f"c_grp{u}") for u, (a, n) in enumerate(UNITS)]
+        c_codes = [keep.tile([P, n], U32, align_bytes=64, name=f"c_codes{u}") for u, (a, n) in enumerate(UNITS)]
+        c_scales = [keep.tile([P, n], U8, align_bytes=64, name=f"c_scales{u}") for u, (a, n) in enumerate(UNITS)]
+        o_sb = [keep.tile([P, 4, n], F32, name=f"o_sb{u}") for u, (a, n) in enumerate(UNITS)]
         out_view = out.rearrange("(f p) t -> p f t", p=P)
-        late, o_banks = {}, {}
+        late = {}
 
-        def round_early(b):
-            round_c(b, 0, early_banks[b // 2][:, b % 2, :], nc.scalar.copy)
+        def combine(i, tag):
+            a, n = GROUPS[i]
+            late[i] = keep.tile([P, 2, 2, n], F32, align_bytes=64, tag=tag, name=f"late{i}")
+            for k in range(2):
+                for q in range(2):
+                    gated(late[i][:, k, q, :], q, 2 + k, a, n)
 
-        def interleave_wp(h):
-            nc.scalar.copy(*line_view(wp_grp[:, h * HALF : (h + 1) * HALF, :], wp_raw[:, :, h * HALF : (h + 1) * HALF]))
+        def turn(u, i, bank_at, engine):
+            a, n = UNITS[u]
+            lo = a - GROUPS[i][0]
+            bank = banks.tile([P, n // P, HALF], F32, name=f"bank{bank_at}")
+            for k in range(2):
+                add_turned(bank, k, [late[i][:, k, q, lo : lo + n] for q in range(2)], n)
+            round_c(u, 1, bank, engine)
+            words = c_rows[u][:].rearrange("t b w p v -> t (b w p v)").bitcast(F32)
+            back = banks.tile([P, n // P, 2, P], F32, name=f"bank{2 + u % 2}")
+            for b in range(n // P):
+                for k in range(2):
+                    nc.tensor.transpose(back[:, b, k, :], words[:, (2 * b + k) * P : (2 * b + k + 1) * P], ident[:])
+            engine(
+                c_grp[u][:].bitcast(F32).rearrange("p (b t w) -> p b t w", t=P, w=2),
+                back[:].rearrange("p b w t -> p b t w"),
+            )
 
-        def combine(b, tag):
-            late[b] = keep.tile([P, 2, 2, P], F32, align_bytes=64, tag=tag, name=f"late{b}")
-            for i in range(2):
-                gated(late[b][:, i, :, :], 2 + i, b * P, P)
-
-        def round_late(b, engine):
-            round_c(b, 1, turn_and_add([late[b][:, 0, :, :], late[b][:, 1, :, :]], P, turns, "late")[:, 0, :], engine)
-
-        def turn_back(b, engine):
-            words = c_rows[b][:].rearrange("t u p v -> t (u p v)").bitcast(F32)
-            bank = banks.tile([P, 2, P], F32, name="bank")
-            for u in range(2):
-                nc.tensor.transpose(bank[:, u, :], words[:, u * P : (u + 1) * P], ident[:])
-            engine(c_grp[b][:].bitcast(F32).rearrange("p (t u) -> p t u", u=2), bank[:].rearrange("p u t -> p t u"))
-
-        def project(b):
-            nc.vector.quantize_mx(out=c_codes[b][:].bitcast(FP8X4), scales=c_scales[b][:], in_=c_grp[b][:])
+        def finish(u, engines):
+            a, n = UNITS[u]
+            nc.vector.quantize_mx(out=c_codes[u][:].bitcast(FP8X4), scales=c_scales[u][:], in_=c_grp[u][:])
             for half in range(2):
-                o_banks[b, half] = banks.tile([P, 2, P], F32, name="bank")
-                for u in range(2):
-                    f = 2 * half + u
+                bank = banks.tile([P, 2, n], F32, name=f"bank{4 + 2 * (u % 2) + half}")
+                for k in range(2):
+                    f = 2 * half + k
                     nc.tensor.matmul_mx(
-                        out=o_banks[b, half][:, u, :],
+                        out=bank[:, k, :],
                         lhsT=wp_codes[:, f * P : (f + 1) * P].bitcast(FP8X4),
                         lhsT_scale=wp_scales[:, f * P : (f + 1) * P],
-                        rhs=c_codes[b][:].bitcast(FP8X4),
-                        rhs_scale=c_scales[b][:],
+                        rhs=c_codes[u][:].bitcast(FP8X4),
+                        rhs_scale=c_scales[u][:],
                         start=True,
                         stop=True,
                     )
-
-        def store(b, engines):
-            cols = slice(b % 2 * P, (b % 2 + 1) * P)
-            for half in range(2):
-                rows = slice(2 * half, 2 * (half + 1))
-                engines[half](o_sb[b // 2][:, rows, cols], o_banks[b, half][:])
-                if b == BLOCKS - 1:
-                    nc.sync.dma_start(out_view[:, rows, b * P : (b + 1) * P], o_sb[b // 2][:, rows, cols])
-            if b == BLOCKS - 2:
-                nc.sync.dma_start(out_view[:, :, b * P : (b + 1) * P], o_sb[b // 2][:, :, cols])
-            elif b % 2 == 1 and b < BLOCKS - 1:
-                nc.sync.dma_start(out_view[:, :, (b - 1) * P : (b + 1) * P], o_sb[b // 2][:])
-
-        def quantise_wp():
-            nc.vector.quantize_mx(
-                out=wp_codes[:].bitcast(FP8X4), scales=wp_scales[:], in_=wp_grp[:].rearrange("p m j -> p (m j)")
-            )
+                rows = slice(2 * half, 2 * half + 2)
+                engines[half](o_sb[u][:, rows, :], bank[:])
+                nc.sync.dma_start(out_view[:, rows, a : a + n], o_sb[u][:, rows, :])
 
         combine(0, "late0")
         combine(1, "late1")
-        combine(2, "late2")
-        round_early(0)
-        round_early(1)
-        interleave_wp(0)
-        round_late(0, nc.scalar.copy)
-        turn_back(0, nc.scalar.copy)
-        interleave_wp(1)
-        quantise_wp()
-        round_late(1, nc.scalar.copy)
-        round_early(2)
-        round_early(3)
-        turn_back(1, nc.scalar.copy)
-        project(0)
-        combine(3, "c_grp0")
-        round_late(2, nc.scalar.copy)
-        turn_back(2, nc.scalar.copy)
-        round_early(4)
-        round_early(5)
-        project(1)
-        combine(4, "c_grp1")
-        round_late(3, nc.scalar.copy)
-        turn_back(3, nc.scalar.copy)
-        store(0, (nc.scalar.copy, nc.scalar.copy))
-        project(2)
-        combine(5, "c_grp2")
-        round_late(4, nc.scalar.copy)
-        turn_back(4, nc.scalar.copy)
-        store(1, (nc.scalar.copy, nc.scalar.copy))
-        store(2, (nc.scalar.copy, nc.scalar.copy))
-        project(3)
-        round_late(5, nc.vector.tensor_copy)
-        store(3, (nc.scalar.copy, nc.scalar.copy))
-        turn_back(5, nc.vector.tensor_copy)
-        project(4)
-        project(5)
-        store(4, (nc.scalar.copy, nc.scalar.copy))
-        store(5, (nc.scalar.copy, nc.vector.tensor_copy))
+        nc.vector.quantize_mx(
+            out=wp_codes[:].bitcast(FP8X4), scales=wp_scales[:], in_=wp_grp[:].rearrange("p m j -> p (m j)")
+        )
+        turn(0, 0, 0, nc.scalar.copy)
+        turn(1, 0, 1, nc.scalar.copy)
+        turn(2, 1, 1, nc.scalar.copy)
+        finish(0, (nc.scalar.copy, nc.scalar.copy))
+        finish(1, (nc.scalar.copy, nc.scalar.copy))
+        combine(2, "c_grp1")
+        turn(3, 2, 1, nc.vector.tensor_copy)
+        finish(2, (nc.scalar.copy, nc.scalar.copy))
+        finish(3, (nc.scalar.copy, nc.vector.tensor_copy))

@@ -80,19 +80,17 @@ def tile_moe_nxt_lin_none_kernel(tc, xT, w, wp, gate, offs, pos1, pos2, out):
         for i, (a, n, v) in enumerate(X_PIECES):
             nc.sync.dma_start(x_raw[i][:], x_view[:, :, a : a + n])
         nc.sync.dma_start(offs_sb[:], offs)
-        nc.sync.dma_start(pos_sb[0][:], pos1)
-        nc.sync.dma_start(pos_sb[1][:], pos2)
         for e in range(E):
             load_w(0, e)
         gate_view = gate[:, 0:P, :].rearrange("g p t -> p g t")
+        nc.sync.dma_start(pos_sb[0][:], pos1)
+        nc.sync.dma_start(gate_sb[:, 0, :], gate_view[:, 0, :])
         load_w(1, 0)
         load_w(1, 1)
-        load_w(1, 2)
-        load_w(1, 3)
-        nc.sync.dma_start(gate_sb[:, 0, :], gate_view[:, 0, :])
-        load_w(1, 4)
+        nc.sync.dma_start(pos_sb[1][:], pos2)
         nc.sync.dma_start(gate_sb[:, 1, :], gate_view[:, 1, :])
-        load_w(1, 5)
+        for e in range(2, E):
+            load_w(1, e)
         nc.sync.dma_start(wp_raw[:], wp.rearrange("(p j) m -> p j m", j=PACK))
 
         nc.gpsimd.memset(x_scales[:], 0)
@@ -182,38 +180,29 @@ def tile_moe_nxt_lin_none_kernel(tc, xT, w, wp, gate, offs, pos1, pos2, out):
         gather_scales(0, keep.tile([P, TRIO], U8, align_bytes=64, name="s_scales0"))
         prepare_w(0, 0, on_scalar, "g0")
         prepare_w(0, 1, on_scalar, "g1")
+        gather_codes(1, on_raw(0, 1, [P, TRIO], U32, "s_codes1"))
         prepare_w(0, 2, on_scalar, "g2")
-        gather_codes(1, on_raw(0, 2, [P, TRIO], U32, "s_codes1"))
         prepare_w(0, 3, on_scalar, "g3")
+        gather_scales(1, on_raw(0, 3, [P, TRIO], U8, "s_scales1"))
         prepare_w(0, 4, on_scalar, "g4")
         prepare_w(0, 5, on_scalar, "g5")
-        gather_scales(1, on_raw(0, 5, [P, TRIO], U8, "s_scales1", skip=64))
         for r in range(2):
-            experts(r, 0)
-            keep_result(r, 0)
+            for g in range(3):
+                experts(r, g)
         for r in range(2):
-            experts(r, 1)
-            experts(r, 2)
-        prepare_w(1, 0, on_scalar, "g0")
-        prepare_w(1, 1, on_scalar, "g1")
-        prepare_w(1, 2, on_scalar, "g2")
-        prepare_w(1, 3, on_vector, "w_last")
-        keep_result(0, 1)
-        keep_result(0, 2, nc.scalar.copy)
-        keep_result(1, 1)
-        keep_result(1, 2)
+            for g in range(3):
+                keep_result(r, g)
+        prepare_w(1, 0, on_vector, "g4")
 
         early = {}
-        early[0, 0] = keep.tile([P, T], F32, align_bytes=64, name="early0_0")
-        gated(early[0, 0][:], 0, 0, 0, T)
-        early[0, 1] = keep.tile([P, T], F32, align_bytes=64, name="early0_1")
-        gated(early[0, 1][:], 1, 0, 0, T)
-        prepare_w(1, 4, on_scalar, "g4")
-        prepare_w(1, 5, on_scalar, "g5")
-        early[1, 0] = on_raw(1, 5, [P, T], F32, "early1_0")
-        gated(early[1, 0][:], 0, 1, 0, T)
-        early[1, 1] = on_raw(1, 5, [P, T], F32, "early1_1", skip=4 * T)
-        gated(early[1, 1][:], 1, 1, 0, T)
+        for q in range(2):
+            early[0, q] = keep.tile([P, T], F32, align_bytes=64, name=f"early0_{q}")
+            gated(early[0, q][:], q, 0, 0, T)
+        for q in range(2):
+            for e in ((1, 2, 3), (4, 5))[q]:
+                prepare_w(1, e, on_scalar, f"g{e}")
+            early[1, q] = on_raw(1, e, [P, T], F32, f"early1_{q}")
+            gated(early[1, q][:], q, 1, 0, T)
         for g in range(3):
             for r in (2, 3):
                 experts(r, g)

@@ -25,11 +25,12 @@ RAW_BYTES = 4 * PACK * HALF
 Y_BYTES = 4 * SLOTS
 X_PIECES = ((0, 512, 344), (512, 256, 168))
 Y_PIN = (5, 4)
-Y_BANK = ((0, 1, 2), (3, 4, 5), (6, 7, 0), (1, 2, 3))
+Y_BANK = ((0, 1, 2), (3, 1, 2), (6, 7, 0), (4, 5, 3))
 WINDOW = 1024
 TRIO = 3 * C
-GROUPS = ((0, 384), (384, 256), (640, 128))
-UNITS = ((0, 256), (256, 128), (384, 256), (640, 128))
+EARLY = ((1, 2), (7, 5))
+GROUPS = ((0, 384), (384, 128), (512, 128), (640, 128))
+UNITS = ((0, 256), (256, 128), (384, 128), (512, 128), (640, 128))
 
 
 def tile_moe_nxt_lin_none_kernel(tc, xT, w, wp, gate, offs, pos1, pos2, out):
@@ -127,12 +128,19 @@ def tile_moe_nxt_lin_none_kernel(tc, xT, w, wp, gate, offs, pos1, pos2, out):
         def on_scalar(grouped, raw):
             nc.scalar.copy(*line_view(grouped, raw))
 
-        def prepare_w(h, e, interleave, tag):
-            grouped = keep.tile([P, HALF, PACK], BF16, align_bytes=64, tag=tag, name=f"w_grp{h}_{e}")
-            interleave(grouped[:], w_raw[h][e][:])
+        w_grp = {}
+
+        def quantise_w(h, e, a, b):
             nc.vector.quantize_mx(
-                out=w_codes[h][e][:].bitcast(FP8X4), scales=w_scales[h][e][:], in_=grouped[:].rearrange("p n j -> p (n j)")
+                out=w_codes[h][e][:, a:b].bitcast(FP8X4),
+                scales=w_scales[h][e][:, a:b],
+                in_=w_grp[h, e][:, a:b, :].rearrange("p n j -> p (n j)"),
             )
+
+        def prepare_w(h, e, interleave, tag, upto=HALF):
+            w_grp[h, e] = keep.tile([P, HALF, PACK], BF16, align_bytes=64, tag=tag, name=f"w_grp{h}_{e}")
+            interleave(w_grp[h, e][:], w_raw[h][e][:])
+            quantise_w(h, e, 0, upto)
 
         y_banks = {}
 
@@ -171,7 +179,6 @@ def tile_moe_nxt_lin_none_kernel(tc, xT, w, wp, gate, offs, pos1, pos2, out):
                         is_transpose=True,
                     )
 
-        c_rows = [keep.tile([P, n // P, 2, P, 2], BF16, align_bytes=64, name=f"c_rows{u}") for u, (a, n) in enumerate(UNITS)]
 
         def round_c(u, h, bank, engine):
             engine(c_rows[u][:, :, :, 64 * h : 64 * (h + 1), :], bank[:].rearrange("t b (m w v) -> t b w m v", w=2, v=2))
@@ -184,13 +191,17 @@ def tile_moe_nxt_lin_none_kernel(tc, xT, w, wp, gate, offs, pos1, pos2, out):
         prepare_w(0, 2, on_scalar, "g2")
         prepare_w(0, 3, on_scalar, "g3")
         gather_scales(1, on_raw(0, 3, [P, TRIO], U8, "s_scales1"))
-        prepare_w(0, 4, on_scalar, "g4")
-        prepare_w(0, 5, on_scalar, "g5")
+        prepare_w(0, 4, on_scalar, "g4", P)
+        prepare_w(0, 5, on_scalar, "g5", P)
+        quantise_w(0, 4, P, HALF)
+        quantise_w(0, 5, P, HALF)
         for r in range(2):
-            for g in range(3):
+            experts(r, 0)
+            keep_result(r, 0)
+        for r in range(2):
+            for g in (1, 2):
                 experts(r, g)
-        for r in range(2):
-            for g in range(3):
+            for g in (1, 2):
                 keep_result(r, g)
         prepare_w(1, 0, on_vector, "g4")
 
@@ -210,12 +221,19 @@ def tile_moe_nxt_lin_none_kernel(tc, xT, w, wp, gate, offs, pos1, pos2, out):
             for r in (2, 3):
                 keep_result(r, g)
         nc.scalar.copy(*line_view(wp_grp[:], wp_raw[:]))
-        early_banks = [banks.tile([P, n // P, HALF], F32, name=f"bank{4 + u}") for u, (a, n) in enumerate(UNITS)]
+        c_rows = [keep.tile([P, 2, 2, P, 2], BF16, align_bytes=64, tag="g5", name="c_rows0")]
+        c_rows = c_rows + [on_raw(1, 4, [P, 1, 2, P, 2], BF16, f"c_rows{u}", skip=1024 * u - 960) for u in (1, 2, 3)]
+        c_rows = c_rows + [keep.tile([P, 1, 2, P, 2], BF16, align_bytes=64, tag="g4", name="c_rows4")]
         for r in range(2):
-            for u, (a, n) in enumerate(UNITS):
-                add_turned(early_banks[u], r, [early[r, q][:, a : a + n] for q in range(2)], n)
-        for u in range(len(UNITS)):
-            round_c(u, 0, early_banks[u], nc.scalar.copy)
+            for at, lo, hi in ((EARLY[r][0], 0, 512), (EARLY[r][1], 512, T)):
+                bank = banks.tile([P, (hi - lo) // P, P], F32, name=f"bank{at}")
+                add_turned(bank, 0, [early[r, q][:, lo:hi] for q in range(2)], hi - lo)
+                for u, (a, n) in enumerate(UNITS):
+                    if lo <= a < hi:
+                        nc.scalar.copy(
+                            c_rows[u][:, :, :, 32 * r : 32 * (r + 1), :],
+                            bank[:, (a - lo) // P : (a - lo + n) // P, :].rearrange("t b (m w v) -> t b w m v", w=2, v=2),
+                        )
 
         c_grp = [keep.tile([P, n * PACK], BF16, align_bytes=64, name=f"c_grp{u}") for u, (a, n) in enumerate(UNITS)]
         c_codes = [keep.tile([P, n], U32, align_bytes=64, name=f"c_codes{u}") for u, (a, n) in enumerate(UNITS)]
@@ -223,6 +241,11 @@ def tile_moe_nxt_lin_none_kernel(tc, xT, w, wp, gate, offs, pos1, pos2, out):
         o_sb = [keep.tile([P, 4, n], F32, name=f"o_sb{u}") for u, (a, n) in enumerate(UNITS)]
         out_view = out.rearrange("(f p) t -> p f t", p=P)
         late = {}
+
+        def quantise_wp():
+            nc.vector.quantize_mx(
+                out=wp_codes[:].bitcast(FP8X4), scales=wp_scales[:], in_=wp_grp[:].rearrange("p m j -> p (m j)")
+            )
 
         def combine(i, tag):
             a, n = GROUPS[i]
@@ -270,15 +293,16 @@ def tile_moe_nxt_lin_none_kernel(tc, xT, w, wp, gate, offs, pos1, pos2, out):
 
         combine(0, "late0")
         combine(1, "late1")
-        nc.vector.quantize_mx(
-            out=wp_codes[:].bitcast(FP8X4), scales=wp_scales[:], in_=wp_grp[:].rearrange("p m j -> p (m j)")
-        )
+        combine(2, "late2")
+        quantise_wp()
         turn(0, 0, 0, nc.scalar.copy)
         turn(1, 0, 1, nc.scalar.copy)
-        turn(2, 1, 1, nc.scalar.copy)
+        turn(2, 1, 0, nc.scalar.copy)
+        turn(3, 2, 1, nc.scalar.copy)
         finish(0, (nc.scalar.copy, nc.scalar.copy))
         finish(1, (nc.scalar.copy, nc.scalar.copy))
-        combine(2, "c_grp1")
-        turn(3, 2, 1, nc.vector.tensor_copy)
+        combine(3, "c_grp1")
         finish(2, (nc.scalar.copy, nc.scalar.copy))
-        finish(3, (nc.scalar.copy, nc.vector.tensor_copy))
+        turn(4, 3, 0, nc.vector.tensor_copy)
+        finish(3, (nc.scalar.copy, nc.scalar.copy))
+        finish(4, (nc.scalar.copy, nc.vector.tensor_copy))

@@ -78,25 +78,28 @@ def tile_moe_nxt_lin_none_kernel(tc, xT, w, wp, gate, offs, pos1, pos2, out):
         def load_w(h, e):
             nc.sync.dma_start(w_raw[h][e][:], w[e].rearrange("(p j) n -> p j n", j=PACK)[:, :, h * HALF : (h + 1) * HALF])
 
+        gate_cols = [keep.tile([P, 2, 8], F32, name=f"gate_cols{i}") for i in range(2)]
+        for i, (a, n, v) in enumerate(X_PIECES):
+            nc.scalar.dma_start(
+                gate_cols[i][:, :, 0 : n // P], gate[:, 0, a : a + n].rearrange("g (p v) -> p g v", p=P)
+            )
+
         for i, (a, n, v) in enumerate(X_PIECES):
             nc.sync.dma_start(x_raw[i][:], x_view[:, :, a : a + n])
         nc.sync.dma_start(offs_sb[:], offs)
         for e in range(E):
             load_w(0, e)
-        gate_view = gate[:, 0:P, :].rearrange("g p t -> p g t")
         nc.sync.dma_start(pos_sb[0][:], pos1)
-        nc.sync.dma_start(gate_sb[:, 0, :], gate_view[:, 0, :])
         load_w(1, 0)
         load_w(1, 1)
         nc.sync.dma_start(pos_sb[1][:], pos2)
-        nc.sync.dma_start(gate_sb[:, 1, :], gate_view[:, 1, :])
         for e in range(2, E):
             load_w(1, e)
         nc.sync.dma_start(wp_raw[:], wp.rearrange("(p j) m -> p j m", j=PACK))
 
+        make_identity(nc, ident[:])
         nc.gpsimd.memset(x_scales[:], 0)
         nc.gpsimd.memset(x_codes[:, T:WINDOW], 0)
-        make_identity(nc, ident[:])
 
         def line_view(grouped, raw):
             return (grouped.rearrange("p (c i) j -> p c j i", i=4), raw.rearrange("p j (c i) -> p c j i", i=4))
@@ -111,6 +114,19 @@ def tile_moe_nxt_lin_none_kernel(tc, xT, w, wp, gate, offs, pos1, pos2, out):
                 scales=x_scales[:, a : a + n],
                 in_=x_grp[i][:].rearrange("p t j -> p (t j)"),
             )
+
+        for q in range(2):
+            bank = banks.tile([P, 4, P], F32, name=f"bank{5 + q}")
+            for v in range(4):
+                nc.tensor.transpose(bank[:, v, :], gate_cols[0][:, q, v : v + 1].to_broadcast([P, P]), ident[:])
+            nc.scalar.copy(gate_sb[:, q, 0:512].rearrange("p (t v) -> p t v", v=4), bank[:].rearrange("p v t -> p t v"))
+        bank = banks.tile([P, 2, 2, P], F32, name="bank7")
+        for q in range(2):
+            for v in range(2):
+                nc.tensor.transpose(bank[:, q, v, :], gate_cols[1][:, q, v : v + 1].to_broadcast([P, P]), ident[:])
+        nc.scalar.copy(
+            gate_sb[:, :, 512:T].rearrange("p q (t v) -> p q t v", v=2), bank[:].rearrange("p q v t -> p q t v")
+        )
 
         s_codes, s_scales = {}, {}
 

@@ -8,10 +8,14 @@ SLOTS = E * C
 P = 128
 PACK = 4
 HALF = N // 2
+RUNS = 8
+RUN = T // RUNS
+GATE_PIECES = ((0, 5), (5, 3))
 
 F32 = mybir.dt.float32
 BF16 = mybir.dt.bfloat16
 U32 = mybir.dt.uint32
+I32 = mybir.dt.int32
 U16 = mybir.dt.uint16
 U8 = mybir.dt.uint8
 FP8X4 = mybir.dt.float8_e4m3fn_x4
@@ -24,13 +28,14 @@ BYTES = 4 * (K * T + E * K * N + N * M + 2 * T + M * T) + 2 * (SLOTS + 2 * T)
 RAW_BYTES = 4 * PACK * HALF
 Y_BYTES = 4 * SLOTS
 X_PIECES = ((0, 512, 344), (512, 256, 168))
-Y_PIN = (5, 4)
-Y_BANK = ((0, 1, 2), (3, 1, 2), (6, 7, 0), (4, 5, 3))
+Y_BANK = ((0, 1, 2), (3, 0, 1), (6, 7, 0), (3, 1, 2))
 WINDOW = 1024
 TRIO = 3 * C
-EARLY = ((1, 2), (7, 5))
-GROUPS = ((0, 384), (384, 128), (512, 128), (640, 128))
-UNITS = ((0, 256), (256, 128), (384, 128), (512, 128), (640, 128))
+EARLY_BANK = (4, 5, 6)
+UNITS = ((0, 256), (256, 256), (512, 128), (640, 128))
+TURN_BANK = (0, 0, 2, 3)
+BACK_BANK = (2, 3, 4, 1)
+OUT_BANK = ((0, 2), (5, 6), (7, 2), (4, 0))
 
 
 def tile_moe_nxt_lin_none_kernel(tc, xT, w, wp, gate, offs, pos1, pos2, out):
@@ -52,57 +57,74 @@ def tile_moe_nxt_lin_none_kernel(tc, xT, w, wp, gate, offs, pos1, pos2, out):
         raw_at, y_at, at = {}, {}, 0
         for h in range(2):
             for e in range(E):
-                if e == Y_PIN[h]:
+                if e == E - 1:
                     y_at[2 * h] = at
                     at = at + Y_BYTES - 64
                 raw_at[h, e] = at
                 at = at + RAW_BYTES
-                if e == Y_PIN[h]:
-                    y_at[2 * h + 1] = at - 64
-                    at = at + Y_BYTES - 64
+            y_at[2 * h + 1] = at - 64
+            at = at + Y_BYTES - 64
 
         def on_raw(h, e, shape, dtype, name, skip=0):
             return placed.tile(shape, dtype, align_bytes=64, offset=raw_at[h, e] + skip, name=name)
 
         w_raw = [[on_raw(h, e, [P, PACK, HALF], F32, f"w_raw{h}_{e}") for e in range(E)] for h in range(2)]
-        w_codes = [[keep.tile([P, HALF], U32, align_bytes=64, name=f"w_codes{h}_{e}") for e in range(E)] for h in range(2)]
+        w_codes = [[keep.tile([P, HALF], U32, align_bytes=64, tag=f"wc{h}_{e}", name=f"w_codes{h}_{e}") for e in range(E)] for h in range(2)]
         w_scales = [[keep.tile([P, HALF], U8, align_bytes=64, name=f"w_scales{h}_{e}") for e in range(E)] for h in range(2)]
-        wp_raw = keep.tile([P, PACK, M], F32, align_bytes=64, name="wp_raw")
-        wp_grp = keep.tile([P, M, PACK], BF16, align_bytes=64, name="wp_grp")
+        wp_raw = [keep.tile([P, PACK, HALF], F32, align_bytes=64, name=f"wp_raw{i}") for i in range(2)]
         wp_codes = keep.tile([P, M], U32, align_bytes=64, name="wp_codes")
         wp_scales = keep.tile([P, M], U8, align_bytes=64, name="wp_scales")
-        gate_sb = keep.tile([P, 2, T], F32, name="gate_sb")
         y = [placed.tile([P, SLOTS], F32, align_bytes=64, offset=y_at[r], name=f"y{r}") for r in range(4)]
         ident = keep.tile([P, P], F32, name="ident")
 
         def load_w(h, e):
             nc.sync.dma_start(w_raw[h][e][:], w[e].rearrange("(p j) n -> p j n", j=PACK)[:, :, h * HALF : (h + 1) * HALF])
 
-        gate_cols = [keep.tile([P, 2, 8], F32, name=f"gate_cols{i}") for i in range(2)]
-        for i, (a, n, v) in enumerate(X_PIECES):
-            nc.scalar.dma_start(
-                gate_cols[i][:, :, 0 : n // P], gate[:, 0, a : a + n].rearrange("g (p v) -> p g v", p=P)
-            )
+        gate_rows = keep.tile([P, P], F32, name="gate_rows")
+        gate_raw = keep.tile([2 * RUNS, RUN], F32, name="gate_raw")
+        nc.sync.dma_start(gate_raw[:], gate[:, 0, :].rearrange("g (b t) -> g b t", t=RUN))
+        nc.vector.memset(gate_rows[:], 0.0)
+        nc.vector.tensor_copy(gate_rows[0 : 2 * RUNS, 0:RUN], gate_raw[:])
 
         for i, (a, n, v) in enumerate(X_PIECES):
             nc.sync.dma_start(x_raw[i][:], x_view[:, :, a : a + n])
         nc.sync.dma_start(offs_sb[:], offs)
         for e in range(E):
             load_w(0, e)
-        nc.sync.dma_start(pos_sb[0][:], pos1)
         load_w(1, 0)
+        nc.sync.dma_start(pos_sb[0][:], pos1)
         load_w(1, 1)
         nc.sync.dma_start(pos_sb[1][:], pos2)
         for e in range(2, E):
             load_w(1, e)
-        nc.sync.dma_start(wp_raw[:], wp.rearrange("(p j) m -> p j m", j=PACK))
+        for i in range(2):
+            nc.sync.dma_start(wp_raw[i][:], wp.rearrange("(p j) m -> p j m", j=PACK)[:, :, i * HALF : (i + 1) * HALF])
 
         make_identity(nc, ident[:])
-        nc.gpsimd.memset(x_scales[:], 0)
-        nc.gpsimd.memset(x_codes[:, T:WINDOW], 0)
+        nc.vector.memset(x_scales[:].bitcast(I32), 0)
+        nc.vector.memset(x_codes[:, T:WINDOW].bitcast(I32), 0)
 
         def line_view(grouped, raw):
             return (grouped.rearrange("p (c i) j -> p c j i", i=4), raw.rearrange("p j (c i) -> p c j i", i=4))
+
+        bank = banks.tile([P, P], F32, name="bank3")
+        nc.tensor.transpose(bank[:], gate_rows[:], ident[:])
+        gate_cols = keep.tile([P, 2 * RUNS], F32, name="gate_cols")
+        nc.vector.tensor_copy(gate_cols[:], bank[:, 0 : 2 * RUNS])
+        gate_banks = {}
+        for q in range(2):
+            for i, (first, count) in enumerate(GATE_PIECES):
+                gate_banks[q, i] = banks.tile([P, 4 * P], F32, name=f"bank{4 + 2 * q + i}")
+                for b in range(count):
+                    col = q * RUNS + first + b
+                    nc.tensor.transpose(
+                        gate_banks[q, i][:, b * RUN : b * RUN + P], gate_cols[:, col : col + 1].to_broadcast([P, P]), ident[:]
+                    )
+        gate_sb = {}
+
+        def spread_gate(q, i):
+            first, count = GATE_PIECES[i]
+            nc.scalar.copy(gate_sb[q][:, first * RUN : (first + count) * RUN], gate_banks[q, i][:, 0 : count * RUN])
 
         for i, (a, n, v) in enumerate(X_PIECES):
             o, s = line_view(x_grp[i][:, 0:v, :], x_raw[i][:, :, 0:v])
@@ -114,19 +136,10 @@ def tile_moe_nxt_lin_none_kernel(tc, xT, w, wp, gate, offs, pos1, pos2, out):
                 scales=x_scales[:, a : a + n],
                 in_=x_grp[i][:].rearrange("p t j -> p (t j)"),
             )
-
+            gate_sb[i] = keep.tile([P, T], F32, tag=f"x_raw{i}", name=f"gate_sb{i}")
+            spread_gate(i, 0)
         for q in range(2):
-            bank = banks.tile([P, 4, P], F32, name=f"bank{5 + q}")
-            for v in range(4):
-                nc.tensor.transpose(bank[:, v, :], gate_cols[0][:, q, v : v + 1].to_broadcast([P, P]), ident[:])
-            nc.scalar.copy(gate_sb[:, q, 0:512].rearrange("p (t v) -> p t v", v=4), bank[:].rearrange("p v t -> p t v"))
-        bank = banks.tile([P, 2, 2, P], F32, name="bank7")
-        for q in range(2):
-            for v in range(2):
-                nc.tensor.transpose(bank[:, q, v, :], gate_cols[1][:, q, v : v + 1].to_broadcast([P, P]), ident[:])
-        nc.scalar.copy(
-            gate_sb[:, :, 512:T].rearrange("p q (t v) -> p q t v", v=2), bank[:].rearrange("p q v t -> p q t v")
-        )
+            spread_gate(q, 1)
 
         s_codes, s_scales = {}, {}
 
@@ -146,17 +159,17 @@ def tile_moe_nxt_lin_none_kernel(tc, xT, w, wp, gate, offs, pos1, pos2, out):
 
         w_grp = {}
 
-        def quantise_w(h, e, a, b):
+        def quantise_w(h, e, a=0, b=HALF):
             nc.vector.quantize_mx(
                 out=w_codes[h][e][:, a:b].bitcast(FP8X4),
                 scales=w_scales[h][e][:, a:b],
                 in_=w_grp[h, e][:, a:b, :].rearrange("p n j -> p (n j)"),
             )
 
-        def prepare_w(h, e, interleave, tag, upto=HALF):
-            w_grp[h, e] = keep.tile([P, HALF, PACK], BF16, align_bytes=64, tag=tag, name=f"w_grp{h}_{e}")
-            interleave(w_grp[h, e][:], w_raw[h][e][:])
-            quantise_w(h, e, 0, upto)
+        def weave_w(h, e, interleave, tag, a=0, b=HALF):
+            if a == 0:
+                w_grp[h, e] = keep.tile([P, HALF, PACK], BF16, align_bytes=64, tag=tag, name=f"w_grp{h}_{e}")
+            interleave(w_grp[h, e][:, a:b, :], w_raw[h][e][:, :, a:b])
 
         y_banks = {}
 
@@ -180,7 +193,7 @@ def tile_moe_nxt_lin_none_kernel(tc, xT, w, wp, gate, offs, pos1, pos2, out):
 
         def gated(part, q, r, a, n):
             nc.vector.tensor_tensor(
-                part, y[r][:].indirect(pos_sb[q][:, a // 16 : (a + n) // 16]), gate_sb[:, q, a : a + n], MULT
+                part, y[r][:].indirect(pos_sb[q][:, a // 16 : (a + n) // 16]), gate_sb[q][:, a : a + n], MULT
             )
 
         def add_turned(bank, i, parts, n):
@@ -196,129 +209,198 @@ def tile_moe_nxt_lin_none_kernel(tc, xT, w, wp, gate, offs, pos1, pos2, out):
                     )
 
 
-        def round_c(u, h, bank, engine):
-            engine(c_rows[u][:, :, :, 64 * h : 64 * (h + 1), :], bank[:].rearrange("t b (m w v) -> t b w m v", w=2, v=2))
+        def round_c(rows, h, bank, engine):
+            engine(rows[:, :, :, 64 * h : 64 * (h + 1), :], bank.rearrange("t b (m w v) -> t b w m v", w=2, v=2))
 
-        gather_codes(0, keep.tile([P, TRIO], U32, align_bytes=64, name="s_codes0"))
-        gather_scales(0, keep.tile([P, TRIO], U8, align_bytes=64, name="s_scales0"))
-        prepare_w(0, 0, on_scalar, "g0")
-        prepare_w(0, 1, on_scalar, "g1")
-        gather_codes(1, on_raw(0, 1, [P, TRIO], U32, "s_codes1"))
-        prepare_w(0, 2, on_scalar, "g2")
-        prepare_w(0, 3, on_scalar, "g3")
-        gather_scales(1, on_raw(0, 3, [P, TRIO], U8, "s_scales1"))
-        prepare_w(0, 4, on_scalar, "g4", P)
-        prepare_w(0, 5, on_scalar, "g5", P)
-        quantise_w(0, 4, P, HALF)
-        quantise_w(0, 5, P, HALF)
-        for r in range(2):
-            experts(r, 0)
-            keep_result(r, 0)
-        for r in range(2):
-            for g in (1, 2):
-                experts(r, g)
-            for g in (1, 2):
-                keep_result(r, g)
-        prepare_w(1, 0, on_vector, "g4")
-
-        early = {}
-        for q in range(2):
-            early[0, q] = keep.tile([P, T], F32, align_bytes=64, name=f"early0_{q}")
-            gated(early[0, q][:], q, 0, 0, T)
-        for q in range(2):
-            for e in ((1, 2, 3), (4, 5))[q]:
-                prepare_w(1, e, on_scalar, f"g{e}")
-            early[1, q] = on_raw(1, e, [P, T], F32, f"early1_{q}")
-            gated(early[1, q][:], q, 1, 0, T)
-        for g in range(3):
-            for r in (2, 3):
-                experts(r, g)
-        for g in range(3):
-            for r in (2, 3):
-                keep_result(r, g)
-        nc.scalar.copy(*line_view(wp_grp[:], wp_raw[:]))
-        c_rows = [keep.tile([P, 2, 2, P, 2], BF16, align_bytes=64, tag="g5", name="c_rows0")]
-        c_rows = c_rows + [on_raw(1, 4, [P, 1, 2, P, 2], BF16, f"c_rows{u}", skip=1024 * u - 960) for u in (1, 2, 3)]
-        c_rows = c_rows + [keep.tile([P, 1, 2, P, 2], BF16, align_bytes=64, tag="g4", name="c_rows4")]
-        for r in range(2):
-            for at, lo, hi in ((EARLY[r][0], 0, 512), (EARLY[r][1], 512, T)):
-                bank = banks.tile([P, (hi - lo) // P, P], F32, name=f"bank{at}")
-                add_turned(bank, 0, [early[r, q][:, lo:hi] for q in range(2)], hi - lo)
-                for u, (a, n) in enumerate(UNITS):
-                    if lo <= a < hi:
-                        nc.scalar.copy(
-                            c_rows[u][:, :, :, 32 * r : 32 * (r + 1), :],
-                            bank[:, (a - lo) // P : (a - lo + n) // P, :].rearrange("t b (m w v) -> t b w m v", w=2, v=2),
-                        )
-
+        on_s, on_v = nc.scalar.copy, nc.vector.tensor_copy
+        c_rows = [keep.tile([P, n // P, 2, P, 2], BF16, align_bytes=64, name=f"c_rows{u}") for u, (a, n) in enumerate(UNITS)]
         c_grp = [keep.tile([P, n * PACK], BF16, align_bytes=64, name=f"c_grp{u}") for u, (a, n) in enumerate(UNITS)]
         c_codes = [keep.tile([P, n], U32, align_bytes=64, name=f"c_codes{u}") for u, (a, n) in enumerate(UNITS)]
         c_scales = [keep.tile([P, n], U8, align_bytes=64, name=f"c_scales{u}") for u, (a, n) in enumerate(UNITS)]
         o_sb = [keep.tile([P, 4, n], F32, name=f"o_sb{u}") for u, (a, n) in enumerate(UNITS)]
         out_view = out.rearrange("(f p) t -> p f t", p=P)
-        late = {}
+        early, early_banks, late, turned, backs, out_banks = {}, {}, {}, {}, {}, {}
+
+        def combine_early(r, q, tile):
+            early[r, q] = tile
+            gated(tile[:], q, r, 0, T)
+
+        def turn_early(r, b):
+            if r == 0:
+                early_banks[b] = banks.tile([P, 2, HALF], F32, name=f"bank{EARLY_BANK[b]}")
+            add_turned(early_banks[b], r, [early[r, q][:, 2 * b * P : 2 * (b + 1) * P] for q in range(2)], 2 * P)
+
+        def round_early(b):
+            for u, (a, n) in enumerate(UNITS):
+                lo, hi = max(a, 2 * b * P), min(a + n, 2 * (b + 1) * P)
+                if lo < hi:
+                    rows = c_rows[u][:, (lo - a) // P : (hi - a) // P]
+                    round_c(rows, 0, early_banks[b][:, lo // P - 2 * b : hi // P - 2 * b, :], on_s)
+
+        def weave_wp(i, engine):
+            engine(*line_view(wp_grp[:, i * HALF : (i + 1) * HALF, :], wp_raw[i][:]))
 
         def quantise_wp():
             nc.vector.quantize_mx(
                 out=wp_codes[:].bitcast(FP8X4), scales=wp_scales[:], in_=wp_grp[:].rearrange("p m j -> p (m j)")
             )
 
-        def combine(i, tag):
-            a, n = GROUPS[i]
-            late[i] = keep.tile([P, 2, 2, n], F32, align_bytes=64, tag=tag, name=f"late{i}")
+        def combine(u, tag):
+            a, n = UNITS[u]
+            late[u] = keep.tile([P, 2, 2, n], F32, align_bytes=64, tag=tag, name=f"late{u}")
             for k in range(2):
                 for q in range(2):
-                    gated(late[i][:, k, q, :], q, 2 + k, a, n)
+                    gated(late[u][:, k, q, :], q, 2 + k, a, n)
 
-        def turn(u, i, bank_at, engine):
+        def turn(u):
             a, n = UNITS[u]
-            lo = a - GROUPS[i][0]
-            bank = banks.tile([P, n // P, HALF], F32, name=f"bank{bank_at}")
+            turned[u] = banks.tile([P, n // P, HALF], F32, name=f"bank{TURN_BANK[u]}")
             for k in range(2):
-                add_turned(bank, k, [late[i][:, k, q, lo : lo + n] for q in range(2)], n)
-            round_c(u, 1, bank, engine)
+                add_turned(turned[u], k, [late[u][:, k, q, :] for q in range(2)], n)
+
+        def round_late(u, engine):
+            a, n = UNITS[u]
+            round_c(c_rows[u][:], 1, turned[u][:], engine)
+
+        def turn_back(u):
+            a, n = UNITS[u]
             words = c_rows[u][:].rearrange("t b w p v -> t (b w p v)").bitcast(F32)
-            back = banks.tile([P, n // P, 2, P], F32, name=f"bank{2 + u % 2}")
+            backs[u] = banks.tile([P, n // P, 2, P], F32, name=f"bank{BACK_BANK[u]}")
             for b in range(n // P):
                 for k in range(2):
-                    nc.tensor.transpose(back[:, b, k, :], words[:, (2 * b + k) * P : (2 * b + k + 1) * P], ident[:])
+                    nc.tensor.transpose(backs[u][:, b, k, :], words[:, (2 * b + k) * P : (2 * b + k + 1) * P], ident[:])
+
+        def group_c(u, engine):
             engine(
                 c_grp[u][:].bitcast(F32).rearrange("p (b t w) -> p b t w", t=P, w=2),
-                back[:].rearrange("p b w t -> p b t w"),
+                backs[u][:].rearrange("p b w t -> p b t w"),
             )
 
-        def finish(u, engines):
-            a, n = UNITS[u]
+        def quantise_c(u):
             nc.vector.quantize_mx(out=c_codes[u][:].bitcast(FP8X4), scales=c_scales[u][:], in_=c_grp[u][:])
-            for half in range(2):
-                bank = banks.tile([P, 2, n], F32, name=f"bank{4 + 2 * (u % 2) + half}")
-                for k in range(2):
-                    f = 2 * half + k
-                    nc.tensor.matmul_mx(
-                        out=bank[:, k, :],
-                        lhsT=wp_codes[:, f * P : (f + 1) * P].bitcast(FP8X4),
-                        lhsT_scale=wp_scales[:, f * P : (f + 1) * P],
-                        rhs=c_codes[u][:].bitcast(FP8X4),
-                        rhs_scale=c_scales[u][:],
-                        start=True,
-                        stop=True,
-                    )
-                rows = slice(2 * half, 2 * half + 2)
-                engines[half](o_sb[u][:, rows, :], bank[:])
-                nc.sync.dma_start(out_view[:, rows, a : a + n], o_sb[u][:, rows, :])
 
+        def project(u, half):
+            a, n = UNITS[u]
+            out_banks[u, half] = banks.tile([P, 2, n], F32, name=f"bank{OUT_BANK[u][half]}")
+            for k in range(2):
+                f = 2 * half + k
+                nc.tensor.matmul_mx(
+                    out=out_banks[u, half][:, k, :],
+                    lhsT=wp_codes[:, f * P : (f + 1) * P].bitcast(FP8X4),
+                    lhsT_scale=wp_scales[:, f * P : (f + 1) * P],
+                    rhs=c_codes[u][:].bitcast(FP8X4),
+                    rhs_scale=c_scales[u][:],
+                    start=True,
+                    stop=True,
+                )
+
+        def store(u, half, engine):
+            a, n = UNITS[u]
+            rows = slice(2 * half, 2 * half + 2)
+            engine(o_sb[u][:, rows, :], out_banks[u, half][:])
+            nc.sync.dma_start(out_view[:, rows, a : a + n], o_sb[u][:, rows, :])
+
+        gather_codes(0, keep.tile([P, TRIO], U32, align_bytes=64, name="s_codes0"))
+        gather_scales(0, keep.tile([P, TRIO], U8, align_bytes=64, name="s_scales0"))
+        for e in (0, 1):
+            weave_w(0, e, on_scalar, f"g{e}")
+            quantise_w(0, e)
+        gather_codes(1, on_raw(0, 1, [P, TRIO], U32, "s_codes1"))
+        for e in (2, 3):
+            weave_w(0, e, on_scalar, f"g{e}")
+            quantise_w(0, e)
+        gather_scales(1, on_raw(0, 3, [P, TRIO], U8, "s_scales1"))
+        experts(0, 0)
+        weave_w(0, 4, on_scalar, "g4")
+        quantise_w(0, 4, 0, P)
+        weave_w(0, 5, on_scalar, "g5", 0, P)
+        quantise_w(0, 5, 0, P)
+        weave_w(0, 5, on_scalar, "g5", P, HALF)
+        experts(1, 0)
+        experts(0, 1)
+        experts(0, 2)
+        quantise_w(0, 4, P, HALF)
+        quantise_w(0, 5, P, HALF)
+        keep_result(0, 0)
+        keep_result(0, 1)
+        keep_result(1, 0)
+        weave_w(1, 0, on_vector, "g4")
+        keep_result(0, 2, on_v)
+        quantise_w(1, 0)
+        experts(1, 1)
+        experts(1, 2)
+        weave_w(1, 1, on_scalar, "g1")
+        keep_result(1, 2)
+
+        combine_early(0, 0, keep.tile([P, T], F32, align_bytes=64, name="early0_0"))
+        keep_result(1, 1, on_v)
+        combine_early(0, 1, keep.tile([P, T], F32, align_bytes=64, name="early0_1"))
+        quantise_w(1, 1)
+        for e in (2, 3):
+            weave_w(1, e, on_scalar, f"g{e}")
+            quantise_w(1, e)
+        for b in range(2):
+            turn_early(0, b)
+        combine_early(1, 0, on_raw(1, 3, [P, T], F32, "early1_0"))
+        for g in (0, 1):
+            for r in (2, 3):
+                experts(r, g)
+        for e in (4, 5):
+            weave_w(1, e, on_scalar, f"g{e}")
+            quantise_w(1, e)
+        combine_early(1, 1, on_raw(1, 5, [P, T], F32, "early1_1", skip=64))
+        for r in (2, 3):
+            experts(r, 2)
+        for r, g in ((2, 0), (2, 1), (3, 0), (2, 2), (3, 1), (3, 2)):
+            keep_result(r, g)
+        turn_early(0, 2)
+        for b in range(3):
+            turn_early(1, b)
+
+        wp_grp = keep.tile([P, M, PACK], BF16, align_bytes=64, tag="wc1_5", name="wp_grp")
+        weave_wp(0, on_s)
+        round_early(0)
+        weave_wp(1, on_s)
         combine(0, "late0")
-        combine(1, "late1")
-        combine(2, "late2")
+        combine(1, "wp_raw0")
+        combine(2, "wp_raw1")
         quantise_wp()
-        turn(0, 0, 0, nc.scalar.copy)
-        turn(1, 0, 1, nc.scalar.copy)
-        turn(2, 1, 0, nc.scalar.copy)
-        turn(3, 2, 1, nc.scalar.copy)
-        finish(0, (nc.scalar.copy, nc.scalar.copy))
-        finish(1, (nc.scalar.copy, nc.scalar.copy))
-        combine(3, "c_grp1")
-        finish(2, (nc.scalar.copy, nc.scalar.copy))
-        turn(4, 3, 0, nc.vector.tensor_copy)
-        finish(3, (nc.scalar.copy, nc.scalar.copy))
-        finish(4, (nc.scalar.copy, nc.vector.tensor_copy))
+        turn(0)
+        round_late(0, on_s)
+        turn_back(0)
+        round_early(1)
+        round_early(2)
+        group_c(0, on_s)
+        turn(1)
+        round_late(1, on_s)
+        turn(2)
+        turn_back(1)
+        quantise_c(0)
+        combine(3, "c_grp0")
+        round_late(2, on_s)
+        project(0, 0)
+        project(0, 1)
+        group_c(1, on_s)
+        turn(3)
+        turn_back(2)
+        store(0, 0, on_s)
+        quantise_c(1)
+        round_late(3, on_v)
+        store(0, 1, on_s)
+        group_c(2, on_s)
+        project(1, 0)
+        project(1, 1)
+        turn_back(3)
+        quantise_c(2)
+        store(1, 0, on_s)
+        project(2, 0)
+        project(2, 1)
+        group_c(3, on_v)
+        quantise_c(3)
+        store(1, 1, on_s)
+        project(3, 0)
+        project(3, 1)
+        store(2, 0, on_v)
+        store(2, 1, on_s)
+        store(3, 0, on_v)
+        store(3, 1, on_s)

@@ -8,9 +8,6 @@ SLOTS = E * C
 P = 128
 PACK = 4
 HALF = N // 2
-RUNS = 8
-RUN = T // RUNS
-GATE_PIECES = ((0, 5), (5, 3))
 
 F32 = mybir.dt.float32
 BF16 = mybir.dt.bfloat16
@@ -28,14 +25,14 @@ BYTES = 4 * (K * T + E * K * N + N * M + 2 * T + M * T) + 2 * (SLOTS + 2 * T)
 RAW_BYTES = 4 * PACK * HALF
 Y_BYTES = 4 * SLOTS
 X_PIECES = ((0, 512, 344), (512, 256, 168))
-Y_BANK = ((0, 1, 2), (3, 0, 1), (6, 7, 0), (3, 1, 2))
+Y_BANK = ((0, 1, 2), (3, 4, 5), (6, 7, 0), (3, 1, 2))
 WINDOW = 1024
 TRIO = 3 * C
 EARLY_BANK = (4, 5, 6)
 UNITS = ((0, 256), (256, 256), (512, 128), (640, 128))
 TURN_BANK = (0, 0, 2, 3)
 BACK_BANK = (2, 3, 4, 1)
-OUT_BANK = ((0, 2), (5, 6), (7, 2), (4, 0))
+OUT_BANK = ((0, 2), (5, 6), (7, 2), (4, 0, 3, 5))
 
 
 def tile_moe_nxt_lin_none_kernel(tc, xT, w, wp, gate, offs, pos1, pos2, out):
@@ -69,8 +66,11 @@ def tile_moe_nxt_lin_none_kernel(tc, xT, w, wp, gate, offs, pos1, pos2, out):
             return placed.tile(shape, dtype, align_bytes=64, offset=raw_at[h, e] + skip, name=name)
 
         w_raw = [[on_raw(h, e, [P, PACK, HALF], F32, f"w_raw{h}_{e}") for e in range(E)] for h in range(2)]
-        w_codes = [[keep.tile([P, HALF], U32, align_bytes=64, tag=f"wc{h}_{e}", name=f"w_codes{h}_{e}") for e in range(E)] for h in range(2)]
-        w_scales = [[keep.tile([P, HALF], U8, align_bytes=64, name=f"w_scales{h}_{e}") for e in range(E)] for h in range(2)]
+        w_codes = [keep.tile([P, HALF], U32, align_bytes=64, tag=f"wc1_{e}", name=f"w_codes{e}") for e in range(E)]
+        w_scales = [keep.tile([P, HALF], U8, align_bytes=64, name=f"w_scales{e}") for e in range(E)]
+        first_grp = [keep.tile([P, E * P, PACK], BF16, align_bytes=64, name=f"first_grp{i}") for i in range(2)]
+        first_codes = [keep.tile([P, E * P], U32, align_bytes=64, name=f"first_codes{i}") for i in range(2)]
+        first_scales = {0: keep.tile([P, E * P], U8, align_bytes=64, name="first_scales0")}
         wp_raw = [keep.tile([P, PACK, HALF], F32, align_bytes=64, name=f"wp_raw{i}") for i in range(2)]
         wp_codes = keep.tile([P, M], U32, align_bytes=64, name="wp_codes")
         wp_scales = keep.tile([P, M], U8, align_bytes=64, name="wp_scales")
@@ -80,21 +80,19 @@ def tile_moe_nxt_lin_none_kernel(tc, xT, w, wp, gate, offs, pos1, pos2, out):
         def load_w(h, e):
             nc.sync.dma_start(w_raw[h][e][:], w[e].rearrange("(p j) n -> p j n", j=PACK)[:, :, h * HALF : (h + 1) * HALF])
 
-        gate_rows = keep.tile([P, P], F32, name="gate_rows")
-        gate_raw = keep.tile([2 * RUNS, RUN], F32, name="gate_raw")
-        nc.sync.dma_start(gate_raw[:], gate[:, 0, :].rearrange("g (b t) -> g b t", t=RUN))
-        nc.vector.memset(gate_rows[:], 0.0)
-        nc.vector.tensor_copy(gate_rows[0 : 2 * RUNS, 0:RUN], gate_raw[:])
+        gate_sb = [keep.tile([P, T], F32, name=f"gate_sb{q}") for q in range(2)]
 
         for i, (a, n, v) in enumerate(X_PIECES):
             nc.sync.dma_start(x_raw[i][:], x_view[:, :, a : a + n])
         nc.sync.dma_start(offs_sb[:], offs)
         for e in range(E):
             load_w(0, e)
-        load_w(1, 0)
         nc.sync.dma_start(pos_sb[0][:], pos1)
-        load_w(1, 1)
+        nc.sync.dma_start(gate_sb[0][:], gate[0, 0:P, :])
+        load_w(1, 0)
         nc.sync.dma_start(pos_sb[1][:], pos2)
+        nc.sync.dma_start(gate_sb[1][:], gate[1, 0:P, :])
+        load_w(1, 1)
         for e in range(2, E):
             load_w(1, e)
         for i in range(2):
@@ -107,25 +105,6 @@ def tile_moe_nxt_lin_none_kernel(tc, xT, w, wp, gate, offs, pos1, pos2, out):
         def line_view(grouped, raw):
             return (grouped.rearrange("p (c i) j -> p c j i", i=4), raw.rearrange("p j (c i) -> p c j i", i=4))
 
-        bank = banks.tile([P, P], F32, name="bank3")
-        nc.tensor.transpose(bank[:], gate_rows[:], ident[:])
-        gate_cols = keep.tile([P, 2 * RUNS], F32, name="gate_cols")
-        nc.vector.tensor_copy(gate_cols[:], bank[:, 0 : 2 * RUNS])
-        gate_banks = {}
-        for q in range(2):
-            for i, (first, count) in enumerate(GATE_PIECES):
-                gate_banks[q, i] = banks.tile([P, 4 * P], F32, name=f"bank{4 + 2 * q + i}")
-                for b in range(count):
-                    col = q * RUNS + first + b
-                    nc.tensor.transpose(
-                        gate_banks[q, i][:, b * RUN : b * RUN + P], gate_cols[:, col : col + 1].to_broadcast([P, P]), ident[:]
-                    )
-        gate_sb = {}
-
-        def spread_gate(q, i):
-            first, count = GATE_PIECES[i]
-            nc.scalar.copy(gate_sb[q][:, first * RUN : (first + count) * RUN], gate_banks[q, i][:, 0 : count * RUN])
-
         for i, (a, n, v) in enumerate(X_PIECES):
             o, s = line_view(x_grp[i][:, 0:v, :], x_raw[i][:, :, 0:v])
             nc.vector.tensor_copy(o, s)
@@ -136,10 +115,6 @@ def tile_moe_nxt_lin_none_kernel(tc, xT, w, wp, gate, offs, pos1, pos2, out):
                 scales=x_scales[:, a : a + n],
                 in_=x_grp[i][:].rearrange("p t j -> p (t j)"),
             )
-            gate_sb[i] = keep.tile([P, T], F32, tag=f"x_raw{i}", name=f"gate_sb{i}")
-            spread_gate(i, 0)
-        for q in range(2):
-            spread_gate(q, 1)
 
         s_codes, s_scales = {}, {}
 
@@ -147,29 +122,33 @@ def tile_moe_nxt_lin_none_kernel(tc, xT, w, wp, gate, offs, pos1, pos2, out):
             s_codes[g] = tile
             nc.vector.tensor_copy(s_codes[g][:], x_codes[:].indirect(offs_sb[:, g * TRIO // 16 : (g + 1) * TRIO // 16]))
 
-        def gather_scales(g, tile):
-            s_scales[g] = tile
-            nc.vector.tensor_copy(s_scales[g][:], x_scales[:].indirect(offs_sb[:, g * TRIO // 16 : (g + 1) * TRIO // 16]))
+        def gather_scales(first, count, tile):
+            for e in range(first, first + count):
+                s_scales[e] = tile[:, (e - first) * C : (e - first + 1) * C]
+            nc.vector.tensor_copy(tile, x_scales[:].indirect(offs_sb[:, first * C // 16 : (first + count) * C // 16]))
 
-        def on_vector(grouped, raw):
-            nc.vector.tensor_copy(*line_view(grouped, raw))
+        def weave_first(e):
+            for i in range(2):
+                nc.scalar.copy(*line_view(first_grp[i][:, e * P : (e + 1) * P, :], w_raw[0][e][:, :, i * P : (i + 1) * P]))
 
-        def on_scalar(grouped, raw):
-            nc.scalar.copy(*line_view(grouped, raw))
+        def quantise_first(i, a, b):
+            nc.vector.quantize_mx(
+                out=first_codes[i][:, a * P : b * P].bitcast(FP8X4),
+                scales=first_scales[i][:, a * P : b * P],
+                in_=first_grp[i][:, a * P : b * P, :].rearrange("p n j -> p (n j)"),
+            )
 
         w_grp = {}
 
-        def quantise_w(h, e, a=0, b=HALF):
-            nc.vector.quantize_mx(
-                out=w_codes[h][e][:, a:b].bitcast(FP8X4),
-                scales=w_scales[h][e][:, a:b],
-                in_=w_grp[h, e][:, a:b, :].rearrange("p n j -> p (n j)"),
-            )
+        def weave_w(e, engine):
+            tag = "first_codes0" if e == 0 else f"w_grp{e}"
+            w_grp[e] = keep.tile([P, HALF, PACK], BF16, align_bytes=64, tag=tag, name=f"w_grp{e}")
+            engine(*line_view(w_grp[e][:], w_raw[1][e][:]))
 
-        def weave_w(h, e, interleave, tag, a=0, b=HALF):
-            if a == 0:
-                w_grp[h, e] = keep.tile([P, HALF, PACK], BF16, align_bytes=64, tag=tag, name=f"w_grp{h}_{e}")
-            interleave(w_grp[h, e][:, a:b, :], w_raw[h][e][:, :, a:b])
+        def quantise_w(e):
+            nc.vector.quantize_mx(
+                out=w_codes[e][:].bitcast(FP8X4), scales=w_scales[e][:], in_=w_grp[e][:].rearrange("p n j -> p (n j)")
+            )
 
         y_banks = {}
 
@@ -178,12 +157,16 @@ def tile_moe_nxt_lin_none_kernel(tc, xT, w, wp, gate, offs, pos1, pos2, out):
             y_banks[r, g] = banks.tile([P, 2 * C], F32, name=f"bank{Y_BANK[r][g]}")
             for half in range(2):
                 e = 2 * g + half
+                if h == 0:
+                    codes, scales = first_codes[i][:, e * P : (e + 1) * P], first_scales[i][:, e * P : (e + 1) * P]
+                else:
+                    codes, scales = w_codes[e][:, i * P : (i + 1) * P], w_scales[e][:, i * P : (i + 1) * P]
                 nc.tensor.matmul_mx(
                     out=y_banks[r, g][:, half * C : (half + 1) * C],
-                    lhsT=w_codes[h][e][:, i * P : (i + 1) * P].bitcast(FP8X4),
-                    lhsT_scale=w_scales[h][e][:, i * P : (i + 1) * P],
+                    lhsT=codes.bitcast(FP8X4),
+                    lhsT_scale=scales,
                     rhs=s_codes[e // 3][:, e % 3 * C : (e % 3 + 1) * C].bitcast(FP8X4),
-                    rhs_scale=s_scales[e // 3][:, e % 3 * C : (e % 3 + 1) * C],
+                    rhs_scale=s_scales[e],
                     start=True,
                     stop=True,
                 )
@@ -279,13 +262,14 @@ def tile_moe_nxt_lin_none_kernel(tc, xT, w, wp, gate, offs, pos1, pos2, out):
         def quantise_c(u):
             nc.vector.quantize_mx(out=c_codes[u][:].bitcast(FP8X4), scales=c_scales[u][:], in_=c_grp[u][:])
 
-        def project(u, half):
+        def project(u, part):
             a, n = UNITS[u]
-            out_banks[u, half] = banks.tile([P, 2, n], F32, name=f"bank{OUT_BANK[u][half]}")
-            for k in range(2):
-                f = 2 * half + k
+            count = 4 // len(OUT_BANK[u])
+            out_banks[u, part] = banks.tile([P, count, n], F32, name=f"bank{OUT_BANK[u][part]}")
+            for k in range(count):
+                f = count * part + k
                 nc.tensor.matmul_mx(
-                    out=out_banks[u, half][:, k, :],
+                    out=out_banks[u, part][:, k, :],
                     lhsT=wp_codes[:, f * P : (f + 1) * P].bitcast(FP8X4),
                     lhsT_scale=wp_scales[:, f * P : (f + 1) * P],
                     rhs=c_codes[u][:].bitcast(FP8X4),
@@ -294,60 +278,58 @@ def tile_moe_nxt_lin_none_kernel(tc, xT, w, wp, gate, offs, pos1, pos2, out):
                     stop=True,
                 )
 
-        def store(u, half, engine):
+        def store(u, part, engine):
             a, n = UNITS[u]
-            rows = slice(2 * half, 2 * half + 2)
-            engine(o_sb[u][:, rows, :], out_banks[u, half][:])
+            count = 4 // len(OUT_BANK[u])
+            rows = slice(count * part, count * (part + 1))
+            engine(o_sb[u][:, rows, :], out_banks[u, part][:])
             nc.sync.dma_start(out_view[:, rows, a : a + n], o_sb[u][:, rows, :])
 
         gather_codes(0, keep.tile([P, TRIO], U32, align_bytes=64, name="s_codes0"))
-        gather_scales(0, keep.tile([P, TRIO], U8, align_bytes=64, name="s_scales0"))
+        gather_scales(0, 3, keep.tile([P, TRIO], U8, align_bytes=64, name="s_scales0")[:])
         for e in (0, 1):
-            weave_w(0, e, on_scalar, f"g{e}")
-            quantise_w(0, e)
+            weave_first(e)
+            quantise_first(0, e, e + 1)
         gather_codes(1, on_raw(0, 1, [P, TRIO], U32, "s_codes1"))
         for e in (2, 3):
-            weave_w(0, e, on_scalar, f"g{e}")
-            quantise_w(0, e)
-        gather_scales(1, on_raw(0, 3, [P, TRIO], U8, "s_scales1"))
-        experts(0, 0)
-        weave_w(0, 4, on_scalar, "g4")
-        quantise_w(0, 4, 0, P)
-        weave_w(0, 5, on_scalar, "g5", 0, P)
-        quantise_w(0, 5, 0, P)
-        weave_w(0, 5, on_scalar, "g5", P, HALF)
-        experts(1, 0)
-        experts(0, 1)
-        experts(0, 2)
-        quantise_w(0, 4, P, HALF)
-        quantise_w(0, 5, P, HALF)
+            weave_first(e)
+            quantise_first(0, e, e + 1)
+        pair = on_raw(0, 3, [P, 2 * C], U8, "s_scales3")
+        gather_scales(3, 1, pair[:, 0:C])
+        gather_scales(4, 1, pair[:, C : 2 * C])
+        weave_first(4)
+        quantise_first(0, 4, 5)
+        gather_scales(5, 1, on_raw(0, 4, [P, C], U8, "s_scales5")[:])
+        weave_first(5)
+        quantise_first(0, 5, 6)
+        for g in range(3):
+            experts(0, g)
+        first_scales[1] = on_raw(0, 5, [P, E * P], U8, "first_scales1", skip=64)
+        quantise_first(1, 0, 4)
+        quantise_first(1, 4, 6)
         keep_result(0, 0)
         keep_result(0, 1)
-        keep_result(1, 0)
-        weave_w(1, 0, on_vector, "g4")
         keep_result(0, 2, on_v)
-        quantise_w(1, 0)
-        experts(1, 1)
-        experts(1, 2)
-        weave_w(1, 1, on_scalar, "g1")
-        keep_result(1, 2)
+        weave_w(0, on_s)
+        for g in range(3):
+            experts(1, g)
+            keep_result(1, g)
 
         combine_early(0, 0, keep.tile([P, T], F32, align_bytes=64, name="early0_0"))
-        keep_result(1, 1, on_v)
         combine_early(0, 1, keep.tile([P, T], F32, align_bytes=64, name="early0_1"))
-        quantise_w(1, 1)
-        for e in (2, 3):
-            weave_w(1, e, on_scalar, f"g{e}")
-            quantise_w(1, e)
+        quantise_w(0)
+        for e in (1, 2):
+            weave_w(e, on_s)
+            quantise_w(e)
         for b in range(2):
             turn_early(0, b)
-        combine_early(1, 0, on_raw(1, 3, [P, T], F32, "early1_0"))
+        combine_early(1, 0, on_raw(1, 2, [P, T], F32, "early1_0"))
+        for e in (3, 4, 5):
+            weave_w(e, on_s)
+            quantise_w(e)
         for g in (0, 1):
             for r in (2, 3):
                 experts(r, g)
-        for e in (4, 5):
-            weave_w(1, e, on_scalar, f"g{e}")
-            quantise_w(1, e)
         combine_early(1, 1, on_raw(1, 5, [P, T], F32, "early1_1", skip=64))
         for r in (2, 3):
             experts(r, 2)
@@ -400,7 +382,11 @@ def tile_moe_nxt_lin_none_kernel(tc, xT, w, wp, gate, offs, pos1, pos2, out):
         store(1, 1, on_s)
         project(3, 0)
         project(3, 1)
+        project(3, 2)
+        project(3, 3)
         store(2, 0, on_v)
         store(2, 1, on_s)
         store(3, 0, on_v)
         store(3, 1, on_s)
+        store(3, 2, on_v)
+        store(3, 3, on_s)

@@ -24,8 +24,13 @@ BYTES = 4 * (K * T + E * K * N + N * M + 2 * T + M * T) + 2 * (SLOTS + 2 * T)
 
 RAW_BYTES = 4 * PACK * HALF
 Y_BYTES = 4 * SLOTS
-X_PIECES = ((0, 512, 344), (512, 256, 168))
-Y_BANK = ((0, 1, 2), (3, 4, 5), (6, 7, 0), (3, 1, 2))
+X_PIECES = ((0, 256, 168), (256, 256, 168), (512, 256, 168))
+Y_GROUPS = (
+    ((0, 2, 0), (2, 2, 1), (4, 1, 2), (5, 1, 5)),
+    ((0, 2, 3), (2, 2, 4), (4, 2, 0)),
+    ((0, 2, 6), (2, 2, 7), (4, 2, 0)),
+    ((0, 2, 3), (2, 2, 1), (4, 2, 2)),
+)
 WINDOW = 1024
 TRIO = 3 * C
 EARLY_BANK = (4, 5, 6)
@@ -154,9 +159,10 @@ def tile_moe_nxt_lin_none_kernel(tc, xT, w, wp, gate, offs, pos1, pos2, out):
 
         def experts(r, g):
             h, i = divmod(r, 2)
-            y_banks[r, g] = banks.tile([P, 2 * C], F32, name=f"bank{Y_BANK[r][g]}")
-            for half in range(2):
-                e = 2 * g + half
+            first, count, bank = Y_GROUPS[r][g]
+            y_banks[r, g] = banks.tile([P, count * C], F32, name=f"bank{bank}")
+            for half in range(count):
+                e = first + half
                 if h == 0:
                     codes, scales = first_codes[i][:, e * P : (e + 1) * P], first_scales[i][:, e * P : (e + 1) * P]
                 else:
@@ -172,7 +178,8 @@ def tile_moe_nxt_lin_none_kernel(tc, xT, w, wp, gate, offs, pos1, pos2, out):
                 )
 
         def keep_result(r, g, engine=nc.scalar.copy):
-            engine(y[r][:, 2 * g * C : 2 * (g + 1) * C], y_banks[r, g][:])
+            first, count, bank = Y_GROUPS[r][g]
+            engine(y[r][:, first * C : (first + count) * C], y_banks[r, g][:])
 
         def gated(part, q, r, a, n):
             nc.vector.tensor_tensor(
@@ -302,15 +309,14 @@ def tile_moe_nxt_lin_none_kernel(tc, xT, w, wp, gate, offs, pos1, pos2, out):
         gather_scales(5, 1, on_raw(0, 4, [P, C], U8, "s_scales5")[:])
         weave_first(5)
         quantise_first(0, 5, 6)
-        for g in range(3):
+        for g in range(4):
             experts(0, g)
         first_scales[1] = on_raw(0, 5, [P, E * P], U8, "first_scales1", skip=64)
         quantise_first(1, 0, 4)
         quantise_first(1, 4, 6)
-        keep_result(0, 0)
-        keep_result(0, 1)
-        keep_result(0, 2, on_v)
-        weave_w(0, on_s)
+        for g in range(4):
+            keep_result(0, g)
+        weave_w(0, on_v)
         for g in range(3):
             experts(1, g)
             keep_result(1, g)

@@ -108,7 +108,7 @@ def tile_moe_nxt_lin_none_kernel(tc, xT, w, wp, gate, offs, pos1, pos2, out):
         nc.vector.memset(x_codes[:, T:WINDOW].bitcast(I32), 0)
 
         def line_view(grouped, raw):
-            return (grouped.rearrange("p (c i) j -> p c j i", i=4), raw.rearrange("p j (c i) -> p c j i", i=4))
+            return (grouped.rearrange("p (c i) j -> p c j i", i=2), raw.rearrange("p j (c i) -> p c j i", i=2))
 
         for i, (a, n, v) in enumerate(X_PIECES):
             o, s = line_view(x_grp[i][:, 0:v, :], x_raw[i][:, :, 0:v])

from contextlib import ExitStack

import concourse.mybir as mybir
from concourse.masks import make_identity

K, T, E, C, N, M = 512, 768, 6, 256, 512, 512
SLOTS = E * C
P = 128
PACK = 4
HALF = N // 2

F32 = mybir.dt.float32
BF16 = mybir.dt.bfloat16
U32 = mybir.dt.uint32
I32 = mybir.dt.int32
U16 = mybir.dt.uint16
U8 = mybir.dt.uint8
FP8X4 = mybir.dt.float8_e4m3fn_x4
MULT = mybir.AluOpType.mult
COPY = mybir.ActivationFunctionType.Copy

FLOPS = 2 * SLOTS * K * N + 2 * T * N * M
BYTES = 4 * (K * T + E * K * N + N * M + 2 * T + M * T) + 2 * (SLOTS + 2 * T)

RAW_BYTES = 4 * PACK * HALF
Y_BYTES = 4 * SLOTS
X_PIECES = ((0, 256, 168), (256, 256, 168), (512, 256, 168))
Y_GROUPS = (
    ((0, 2, 0), (2, 2, 1), (4, 1, 2), (5, 1, 5)),
    ((0, 2, 3), (2, 2, 4), (4, 2, 0)),
    ((0, 2, 6), (2, 2, 7), (4, 2, 0)),
    ((0, 2, 3), (2, 2, 1), (4, 2, 2)),
)
WINDOW = 1024
TRIO = 3 * C
EARLY_BANK = (4, 5, 6)
UNITS = ((0, 256), (256, 256), (512, 128), (640, 128))
TURN_BANK = (0, 0, 2, 3)
BACK_BANK = (2, 3, 4, 1)
OUT_BANK = ((0, 2), (5, 6), (7, 2), (4, 0, 3, 5))


def tile_moe_nxt_lin_none_kernel(tc, xT, w, wp, gate, offs, pos1, pos2, out):
    nc = tc.nc
    with ExitStack() as ctx:
        lists = ctx.enter_context(tc.tile_pool(name="lists", bufs=1))
        keep = ctx.enter_context(tc.tile_pool(name="keep", bufs=1))
        placed = ctx.enter_context(tc.tile_pool(name="placed", bufs=1))
        banks = ctx.enter_context(tc.psum_pool(name="banks", bufs=1))

        offs_sb = lists.tile([P, SLOTS // 16], U16, name="offs_sb")
        pos_sb = [lists.tile([P, T // 16], U16, name=f"pos{q}_sb") for q in range(2)]

        x_view = xT.rearrange("(p j) t -> p j t", j=PACK)
        x_raw = [keep.tile([P, PACK, n], F32, name=f"x_raw{i}") for i, (a, n, v) in enumerate(X_PIECES)]
        x_grp = [keep.tile([P, n, PACK], BF16, align_bytes=64, name=f"x_grp{i}") for i, (a, n, v) in enumerate(X_PIECES)]
        x_codes = keep.tile([P, WINDOW], U32, align_bytes=64, name="x_codes")
        x_scales = keep.tile([P, WINDOW], U8, align_bytes=64, name="x_scales")
        raw_at, y_at, at = {}, {}, 0
        for h in range(2):
            for e in range(E):
                if e == E - 1:
                    y_at[2 * h] = at
                    at = at + Y_BYTES - 64
                raw_at[h, e] = at
                at = at + RAW_BYTES
            y_at[2 * h + 1] = at - 64
            at = at + Y_BYTES - 64

        def on_raw(h, e, shape, dtype, name, skip=0):
            return placed.tile(shape, dtype, align_bytes=64, offset=raw_at[h, e] + skip, name=name)

        w_raw = [[on_raw(h, e, [P, PACK, HALF], F32, f"w_raw{h}_{e}") for e in range(E)] for h in range(2)]
        w_codes = [keep.tile([P, HALF], U32, align_bytes=64, tag=f"wc1_{e}", name=f"w_codes{e}") for e in range(E)]
        w_scales = [keep.tile([P, HALF], U8, align_bytes=64, name=f"w_scales{e}") for e in range(E)]
        first_grp = [keep.tile([P, E * P, PACK], BF16, align_bytes=64, name=f"first_grp{i}") for i in range(2)]
        first_codes = [keep.tile([P, E * P], U32, align_bytes=64, name=f"first_codes{i}") for i in range(2)]
        first_scales = {0: keep.tile([P, E * P], U8, align_bytes=64, name="first_scales0")}
        wp_raw = [keep.tile([P, PACK, HALF], F32, align_bytes=64, name=f"wp_raw{i}") for i in range(2)]
        wp_codes = keep.tile([P, M], U32, align_bytes=64, name="wp_codes")
        wp_scales = keep.tile([P, M], U8, align_bytes=64, name="wp_scales")
        y = [placed.tile([P, SLOTS], F32, align_bytes=64, offset=y_at[r], name=f"y{r}") for r in range(4)]
        ident = keep.tile([P, P], F32, name="ident")

        def load_w(h, e):
            nc.sync.dma_start(w_raw[h][e][:], w[e].rearrange("(p j) n -> p j n", j=PACK)[:, :, h * HALF : (h + 1) * HALF])

        gate_sb = [keep.tile([P, T], F32, name=f"gate_sb{q}") for q in range(2)]

        for i, (a, n, v) in enumerate(X_PIECES):
            nc.sync.dma_start(x_raw[i][:], x_view[:, :, a : a + n])
        nc.sync.dma_start(offs_sb[:], offs)
        for e in range(E):
            load_w(0, e)
        nc.sync.dma_start(pos_sb[0][:], pos1)
        nc.sync.dma_start(gate_sb[0][:], gate[0, 0:P, :])
        load_w(1, 0)
        nc.sync.dma_start(pos_sb[1][:], pos2)
        nc.sync.dma_start(gate_sb[1][:], gate[1, 0:P, :])
        load_w(1, 1)
        for e in range(2, E):
            load_w(1, e)
        for i in range(2):
            nc.sync.dma_start(wp_raw[i][:], wp.rearrange("(p j) m -> p j m", j=PACK)[:, :, i * HALF : (i + 1) * HALF])

        make_identity(nc, ident[:])
        nc.vector.memset(x_scales[:].bitcast(I32), 0)
        nc.vector.memset(x_codes[:, T:WINDOW].bitcast(I32), 0)

        def line_view(grouped, raw):
            return (grouped.rearrange("p (c i) j -> p c j i", i=2), raw.rearrange("p j (c i) -> p c j i", i=2))

        for i, (a, n, v) in enumerate(X_PIECES):
            o, s = line_view(x_grp[i][:, 0:v, :], x_raw[i][:, :, 0:v])
            nc.vector.tensor_copy(o, s)
            o, s = line_view(x_grp[i][:, v:n, :], x_raw[i][:, :, v:n])
            nc.scalar.activation(o, s, COPY)
            nc.vector.quantize_mx(
                out=x_codes[:, a : a + n].bitcast(FP8X4),
                scales=x_scales[:, a : a + n],
                in_=x_grp[i][:].rearrange("p t j -> p (t j)"),
            )

        s_codes, s_scales = {}, {}

        def gather_codes(g, tile):
            s_codes[g] = tile
            nc.vector.tensor_copy(s_codes[g][:], x_codes[:].indirect(offs_sb[:, g * TRIO // 16 : (g + 1) * TRIO // 16]))

        def gather_scales(first, count, tile):
            for e in range(first, first + count):
                s_scales[e] = tile[:, (e - first) * C : (e - first + 1) * C]
            nc.vector.tensor_copy(tile, x_scales[:].indirect(offs_sb[:, first * C // 16 : (first + count) * C // 16]))

        def weave_first(e):
            for i in range(2):
                nc.scalar.copy(*line_view(first_grp[i][:, e * P : (e + 1) * P, :], w_raw[0][e][:, :, i * P : (i + 1) * P]))

        def quantise_first(i, a, b):
            nc.vector.quantize_mx(
                out=first_codes[i][:, a * P : b * P].bitcast(FP8X4),
                scales=first_scales[i][:, a * P : b * P],
                in_=first_grp[i][:, a * P : b * P, :].rearrange("p n j -> p (n j)"),
            )

        w_grp = {}

        def weave_w(e, engine):
            tag = "first_codes0" if e == 0 else f"w_grp{e}"
            w_grp[e] = keep.tile([P, HALF, PACK], BF16, align_bytes=64, tag=tag, name=f"w_grp{e}")
            engine(*line_view(w_grp[e][:], w_raw[1][e][:]))

        def quantise_w(e):
            nc.vector.quantize_mx(
                out=w_codes[e][:].bitcast(FP8X4), scales=w_scales[e][:], in_=w_grp[e][:].rearrange("p n j -> p (n j)")
            )

        y_banks = {}

        def experts(r, g):
            h, i = divmod(r, 2)
            first, count, bank = Y_GROUPS[r][g]
            y_banks[r, g] = banks.tile([P, count * C], F32, name=f"bank{bank}")
            for half in range(count):
                e = first + half
                if h == 0:
                    codes, scales = first_codes[i][:, e * P : (e + 1) * P], first_scales[i][:, e * P : (e + 1) * P]
                else:
                    codes, scales = w_codes[e][:, i * P : (i + 1) * P], w_scales[e][:, i * P : (i + 1) * P]
                nc.tensor.matmul_mx(
                    out=y_banks[r, g][:, half * C : (half + 1) * C],
                    lhsT=codes.bitcast(FP8X4),
                    lhsT_scale=scales,
                    rhs=s_codes[e // 3][:, e % 3 * C : (e % 3 + 1) * C].bitcast(FP8X4),
                    rhs_scale=s_scales[e],
                    start=True,
                    stop=True,
                )

        def keep_result(r, g, engine=nc.scalar.copy):
            first, count, bank = Y_GROUPS[r][g]
            engine(y[r][:, first * C : (first + count) * C], y_banks[r, g][:])

        def gated(part, q, r, a, n):
            nc.vector.tensor_tensor(
                part, y[r][:].indirect(pos_sb[q][:, a // 16 : (a + n) // 16]), gate_sb[q][:, a : a + n], MULT
            )

        def add_turned(bank, i, parts, n):
            for b in range(n // P):
                for q in range(2):
                    nc.tensor.matmul(
                        bank[:, b, i * P : (i + 1) * P],
                        parts[q][:, b * P : (b + 1) * P],
                        ident[:],
                        start=(q == 0),
                        stop=(q == 1),
                        is_transpose=True,
                    )


        def round_c(rows, h, bank, engine):
            engine(rows[:, :, :, 64 * h : 64 * (h + 1), :], bank.rearrange("t b (m w v) -> t b w m v", w=2, v=2))

        on_s, on_v = nc.scalar.copy, nc.vector.tensor_copy
        c_rows = [keep.tile([P, n // P, 2, P, 2], BF16, align_bytes=64, name=f"c_rows{u}") for u, (a, n) in enumerate(UNITS)]
        c_grp = [keep.tile([P, n * PACK], BF16, align_bytes=64, name=f"c_grp{u}") for u, (a, n) in enumerate(UNITS)]
        c_codes = [keep.tile([P, n], U32, align_bytes=64, name=f"c_codes{u}") for u, (a, n) in enumerate(UNITS)]
        c_scales = [keep.tile([P, n], U8, align_bytes=64, name=f"c_scales{u}") for u, (a, n) in enumerate(UNITS)]
        o_sb = [keep.tile([P, 4, n], F32, name=f"o_sb{u}") for u, (a, n) in enumerate(UNITS)]
        out_view = out.rearrange("(f p) t -> p f t", p=P)
        early, early_banks, late, turned, backs, out_banks = {}, {}, {}, {}, {}, {}

        def combine_early(r, q, tile):
            early[r, q] = tile
            gated(tile[:], q, r, 0, T)

        def turn_early(r, b):
            if r == 0:
                early_banks[b] = banks.tile([P, 2, HALF], F32, name=f"bank{EARLY_BANK[b]}")
            add_turned(early_banks[b], r, [early[r, q][:, 2 * b * P : 2 * (b + 1) * P] for q in range(2)], 2 * P)

        def round_early(b):
            for u, (a, n) in enumerate(UNITS):
                lo, hi = max(a, 2 * b * P), min(a + n, 2 * (b + 1) * P)
                if lo < hi:
                    rows = c_rows[u][:, (lo - a) // P : (hi - a) // P]
                    round_c(rows, 0, early_banks[b][:, lo // P - 2 * b : hi // P - 2 * b, :], on_s)

        def weave_wp(i, engine):
            engine(*line_view(wp_grp[:, i * HALF : (i + 1) * HALF, :], wp_raw[i][:]))

        def quantise_wp():
            nc.vector.quantize_mx(
                out=wp_codes[:].bitcast(FP8X4), scales=wp_scales[:], in_=wp_grp[:].rearrange("p m j -> p (m j)")
            )

        def combine(u, tag):
            a, n = UNITS[u]
            late[u] = keep.tile([P, 2, 2, n], F32, align_bytes=64, tag=tag, name=f"late{u}")
            for k in range(2):
                for q in range(2):
                    gated(late[u][:, k, q, :], q, 2 + k, a, n)

        def turn(u):
            a, n = UNITS[u]
            turned[u] = banks.tile([P, n // P, HALF], F32, name=f"bank{TURN_BANK[u]}")
            for k in range(2):
                add_turned(turned[u], k, [late[u][:, k, q, :] for q in range(2)], n)

        def round_late(u, engine):
            a, n = UNITS[u]
            round_c(c_rows[u][:], 1, turned[u][:], engine)

        def turn_back(u):
            a, n = UNITS[u]
            words = c_rows[u][:].rearrange("t b w p v -> t (b w p v)").bitcast(F32)
            backs[u] = banks.tile([P, n // P, 2, P], F32, name=f"bank{BACK_BANK[u]}")
            for b in range(n // P):
                for k in range(2):
                    nc.tensor.transpose(backs[u][:, b, k, :], words[:, (2 * b + k) * P : (2 * b + k + 1) * P], ident[:])

        def group_c(u, engine):
            engine(
                c_grp[u][:].bitcast(F32).rearrange("p (b t w) -> p b t w", t=P, w=2),
                backs[u][:].rearrange("p b w t -> p b t w"),
            )

        def quantise_c(u):
            nc.vector.quantize_mx(out=c_codes[u][:].bitcast(FP8X4), scales=c_scales[u][:], in_=c_grp[u][:])

        def project(u, part):
            a, n = UNITS[u]
            count = 4 // len(OUT_BANK[u])
            out_banks[u, part] = banks.tile([P, count, n], F32, name=f"bank{OUT_BANK[u][part]}")
            for k in range(count):
                f = count * part + k
                nc.tensor.matmul_mx(
                    out=out_banks[u, part][:, k, :],
                    lhsT=wp_codes[:, f * P : (f + 1) * P].bitcast(FP8X4),
                    lhsT_scale=wp_scales[:, f * P : (f + 1) * P],
                    rhs=c_codes[u][:].bitcast(FP8X4),
                    rhs_scale=c_scales[u][:],
                    start=True,
                    stop=True,
                )

        def store(u, part, engine):
            a, n = UNITS[u]
            count = 4 // len(OUT_BANK[u])
            rows = slice(count * part, count * (part + 1))
            engine(o_sb[u][:, rows, :], out_banks[u, part][:])
            nc.sync.dma_start(out_view[:, rows, a : a + n], o_sb[u][:, rows, :])

        gather_codes(0, keep.tile([P, TRIO], U32, align_bytes=64, name="s_codes0"))
        gather_scales(0, 3, keep.tile([P, TRIO], U8, align_bytes=64, name="s_scales0")[:])
        for e in (0, 1):
            weave_first(e)
            quantise_first(0, e, e + 1)
        gather_codes(1, on_raw(0, 1, [P, TRIO], U32, "s_codes1"))
        for e in (2, 3):
            weave_first(e)
            quantise_first(0, e, e + 1)
        pair = on_raw(0, 3, [P, 2 * C], U8, "s_scales3")
        gather_scales(3, 1, pair[:, 0:C])
        gather_scales(4, 1, pair[:, C : 2 * C])
        weave_first(4)
        quantise_first(0, 4, 5)
        gather_scales(5, 1, on_raw(0, 4, [P, C], U8, "s_scales5")[:])
        weave_first(5)
        quantise_first(0, 5, 6)
        for g in range(4):
            experts(0, g)
        first_scales[1] = on_raw(0, 5, [P, E * P], U8, "first_scales1", skip=64)
        quantise_first(1, 0, 4)
        quantise_first(1, 4, 6)
        for g in range(4):
            keep_result(0, g)
        weave_w(0, on_v)
        for g in range(3):
            experts(1, g)
            keep_result(1, g)

        combine_early(0, 0, keep.tile([P, T], F32, align_bytes=64, name="early0_0"))
        combine_early(0, 1, keep.tile([P, T], F32, align_bytes=64, name="early0_1"))
        quantise_w(0)
        for e in (1, 2):
            weave_w(e, on_s)
            quantise_w(e)
        for b in range(2):
            turn_early(0, b)
        combine_early(1, 0, on_raw(1, 2, [P, T], F32, "early1_0"))
        for e in (3, 4, 5):
            weave_w(e, on_s)
            quantise_w(e)
        for g in (0, 1):
            for r in (2, 3):
                experts(r, g)
        combine_early(1, 1, on_raw(1, 5, [P, T], F32, "early1_1", skip=64))
        for r in (2, 3):
            experts(r, 2)
        for r, g in ((2, 0), (2, 1), (3, 0), (2, 2), (3, 1), (3, 2)):
            keep_result(r, g)
        turn_early(0, 2)
        for b in range(3):
            turn_early(1, b)

        wp_grp = keep.tile([P, M, PACK], BF16, align_bytes=64, tag="wc1_5", name="wp_grp")
        weave_wp(0, on_s)
        round_early(0)
        weave_wp(1, on_s)
        combine(0, "late0")
        combine(1, "wp_raw0")
        combine(2, "wp_raw1")
        quantise_wp()
        turn(0)
        round_late(0, on_s)
        turn_back(0)
        round_early(1)
        round_early(2)
        group_c(0, on_s)
        turn(1)
        round_late(1, on_s)
        turn(2)
        turn_back(1)
        quantise_c(0)
        combine(3, "c_grp0")
        round_late(2, on_s)
        project(0, 0)
        project(0, 1)
        group_c(1, on_s)
        turn(3)
        turn_back(2)
        store(0, 0, on_s)
        quantise_c(1)
        round_late(3, on_v)
        store(0, 1, on_s)
        group_c(2, on_s)
        project(1, 0)
        project(1, 1)
        turn_back(3)
        quantise_c(2)
        store(1, 0, on_s)
        project(2, 0)
        project(2, 1)
        group_c(3, on_v)
        quantise_c(3)
        store(1, 1, on_s)
        project(3, 0)
        project(3, 1)
        project(3, 2)
        project(3, 3)
        store(2, 0, on_v)
        store(2, 1, on_s)
        store(3, 0, on_v)
        store(3, 1, on_s)
        store(3, 2, on_v)
        store(3, 3, on_s)
